import numpy as np
import ml_dtypes


def mxq(x, axis, fmt="e4m3"):
    dtype, down = {"e4m3": (ml_dtypes.float8_e4m3fn, 7), "e5m2": (ml_dtypes.float8_e5m2, 14)}[fmt]
    v = np.moveaxis(np.asarray(x, np.float32).astype(ml_dtypes.bfloat16).astype(np.float64), axis, -1)
    blocks = v.reshape(v.shape[:-1] + (-1, 32))
    amax = np.abs(blocks).max(-1, keepdims=True)
    byte = np.maximum(np.where(amax > 0, np.frexp(amax)[1] - 1 + 127, 0) - down, 1)
    scale = np.exp2(byte - 127.0)
    codes = (blocks / scale).astype(np.float32).astype(dtype).astype(np.float64)
    return np.moveaxis((codes * scale).reshape(v.shape), -1, axis)


WIDE = False


def mx_kscale(k):
    if not WIDE:
        return np.ones(k)
    levels = np.array([10, -10, 5, -5, 0])
    if k % 512:
        return np.exp2(np.random.permutation(np.resize(levels, k // 32))).repeat(32)
    a = np.empty((k // 512, 16))
    for p in range(k // 512):
        a[p, :8] = np.random.permutation(np.resize(levels, 8))
        for g in range(8):
            far = levels[np.abs(levels - a[p, g]) >= 10]
            a[p, g + 8] = far[np.random.randint(len(far))]
    return np.exp2(a.ravel()).repeat(32)


def f64(x):
    return np.asarray(x).astype(np.float64)


def striped(idx):
    return np.tile(idx.reshape(-1, 16).T, (8, 1)).astype(np.uint16)


def unstriped(offs):
    return offs[:16].T.reshape(-1).astype(np.int64)


E2M1 = np.array([0.0, 0.5, 1.0, 1.5, 2.0, 3.0, 4.0, 6.0, -0.0, -0.5, -1.0, -1.5, -2.0, -3.0, -4.0, -6.0])


def pack_weight(w, fmt):
    k, n = w.shape
    w = f64(np.asarray(w, np.float32).astype(ml_dtypes.bfloat16)).reshape(k // 32, 32, n)
    amax = np.abs(w).max(1)
    if fmt == "e4m3":
        byte = np.frexp(amax)[1] - 1 + 127 - 7
    else:
        mant, ex = np.frexp(amax / 6.0)
        byte = np.where(mant > 0.5, ex, ex - 1) + 127
    byte = np.clip(np.where(amax > 0, byte, 1), 1, 254)
    scaled = (w * np.exp2(127.0 - byte)[:, None, :]).reshape(k, n).astype(np.float32)
    by_word = np.ascontiguousarray(scaled.reshape(k // 512, 128, 4, n).transpose(0, 1, 3, 2))
    if fmt == "e4m3":
        words = by_word.astype(ml_dtypes.float8_e4m3fn).view(np.uint8)
    else:
        c = by_word.astype(ml_dtypes.float4_e2m1fn).view(np.uint8) & 0xF
        words = (c[..., 0::2] | (c[..., 1::2] << 4)).reshape(k // 512, 128, 2 * n)
    return np.ascontiguousarray(words), np.ascontiguousarray(byte.astype(np.uint8).reshape(k // 512, 16, n))


def unpack_weight(words, scales, fmt):
    g, _, n = scales.shape
    words = np.ascontiguousarray(words).reshape(g, 128, n, -1)
    if fmt == "e4m3":
        vals = words.view(ml_dtypes.float8_e4m3fn).astype(np.float64)
    else:
        nib = np.empty((g, 128, n, 4), np.uint8)
        nib[..., 0::2] = words & 0xF
        nib[..., 1::2] = words >> 4
        vals = E2M1[nib]
    vals = vals * np.repeat(np.exp2(scales.astype(np.float64) - 127.0), 8, axis=1)[..., None]
    return vals.transpose(0, 1, 3, 2).reshape(g * 512, n)


def gelu(v):
    return 0.5 * v * (1.0 + np.tanh(np.sqrt(2.0 / np.pi) * (v + 0.044715 * v**3)))


def striped8(idx):
    return np.concatenate([v.reshape(-1, 16).T for v in idx]).astype(np.uint16)


def unstriped8(offs):
    return np.stack([offs[16 * g:16 * g + 16].T.reshape(-1) for g in range(8)]).astype(np.int64)


def heads(xT, wgt, idx8):
    k = np.arange(xT.shape[0])
    return wgt[k // 4 % 128] * xT[k[:, None], idx8[k % 512 // 64]]


K, C, H, N, P, T, S, G, R = 1024, 512, 1024, 512, 2048, 2048, 1024, 8, 16

def setup_inputs():
    n = np.random.standard_normal
    a = mx_kscale(K)[:, None]
    s = mx_kscale(C)[:, None]
    u = mx_kscale(H)[:, None]
    tab_words, tab_scales = pack_weight(n((C, T)) * s, "e4m3")
    w4_words, w4_scales = pack_weight(n((C, H)) / np.sqrt(C) / s, "e2m1")
    return {
        "xT": (n((K, P)) * a).astype(np.float32),
        "wgt": np.repeat(np.random.uniform(0.5, 2.0, (G, S)), R, axis=0).astype(np.float32),
        "offs2": striped8(np.stack([np.random.permutation(P)[:S] for _ in range(G)])),
        "tab_words": tab_words, "tab_scales": tab_scales,
        "offs": striped(np.random.permutation(T)[:S]),
        "wf": (n((K, H)) / np.sqrt(K) / a).astype(np.float32),
        "w4_words": w4_words, "w4_scales": w4_scales,
        "gain": (2.0 * np.exp(0.3 * n(H)) * u[:, 0]).astype(np.float32),
        "ws": (n((H, N)) / np.sqrt(H) / u).astype(np.float32),
        "skip": n((N, S)).astype(np.float32),
    }

def reference(xT, wgt, offs2, tab_words, tab_scales, offs, wf, w4_words, w4_scales, gain, ws, skip):
    xg = mxq(heads(f64(xT), f64(wgt), unstriped8(offs2)), 0, "e4m3")
    v = unpack_weight(tab_words, tab_scales, "e4m3")[:, unstriped(offs)]
    w4 = unpack_weight(w4_words, w4_scales, "e2m1")
    f = mxq(f64(wf), 0, "e4m3").T @ xg
    b = w4.T @ v
    gate = 1.0 / (1.0 + np.exp(-b))
    h = f64(gain)[:, None] * (np.tanh(f) * gate)
    y = mxq(f64(ws), 0, "e4m3").T @ mxq(h, 0, "e4m3")
    return f64(skip) + y

@@ -1,0 +1,391 @@
+from contextlib import ExitStack
+
+import concourse.mybir as mybir
+
+K, C, H, N, T, S = 1024, 512, 1024, 512, 2048, 1024
+FLOPS = 2 * S * (K * H + C * H + H * N)
+
+F32 = mybir.dt.float32
+BF16 = mybir.dt.bfloat16
+I32 = mybir.dt.int32
+U32 = mybir.dt.uint32
+U16 = mybir.dt.uint16
+U8 = mybir.dt.uint8
+FP8X4 = mybir.dt.float8_e4m3fn_x4
+FP4X4 = mybir.dt.float4_e2m1fn_x4
+MULT = mybir.AluOpType.mult
+ADD = mybir.AluOpType.add
+ACT = mybir.ActivationFunctionType
+
+P = 128
+PACK = 4
+PASS = P * PACK
+HALF = 512
+CHUNK = 256
+BIG_BUFS = 12
+ACC_BUFS = 2
+PICKED_BUFS = 3
+GROUPED_BUFS = 4
+FILT_BUFS = 2
+
+
+def tile_list_vocoder_speaker_gate_skip_kernel(
+    tc, xT, wgt, offs2, tab_words, tab_scales, offs, wf, w4_words, w4_scales, gain, ws, skip, out
+):
+    nc = tc.nc
+    with ExitStack() as ctx:
+        keep = ctx.enter_context(tc.tile_pool(name="keep", bufs=1))
+        big = ctx.enter_context(tc.tile_pool(name="big", bufs=BIG_BUFS))
+        stage = ctx.enter_context(tc.tile_pool(name="stage", bufs=3))
+        psum = ctx.enter_context(tc.psum_pool(name="psum", bufs=1))
+
+        def kept(shape, dtype, name):
+            return keep.tile(shape, dtype, name=name, align_bytes=64)
+
+        def loaded(shape, dtype, name, source):
+            tile = big.tile(shape, dtype, name=name, tag="big", align_bytes=64)
+            nc.sync.dma_start(out=tile[:], in_=source)
+            return tile
+
+        offs_sb = kept([P, S // 16], U16, "offs_sb")
+        offs2_sb = kept([P, S // 16], U16, "offs2_sb")
+        tab_plane = kept([P, T // 4], I32, "tab_plane")
+        w4_plane = kept([P, H // 4], I32, "w4_plane")
+        w4_raw = kept([P, H // 2], I32, "w4_raw")
+        wgt_sb = kept([P, S], F32, "wgt_sb")
+        gain_sb = [kept([P, PACK], F32, "gain%d" % b) for b in range(2)]
+
+        x_planes = xT.rearrange("(a p i) t -> a i p t", a=2, i=PACK)
+        wf_rows = wf.rearrange("(a p i) r -> a p i r", a=2, i=PACK)
+        ws_rows = ws.rearrange("(b p i) n -> b p i n", b=2, i=PACK)
+        skip_rows = skip.rearrange("(c p) j -> p c j", p=P)
+        out_rows = out.rearrange("(c p) j -> p c j", p=P)
+
+        tab_sb, x_sb, wf_raw, ws_raw, skip_sb = {}, {}, {}, {}, {}
+
+        def load_x(a, i):
+            x_sb[a, i] = loaded([P, T], F32, "x%d%d" % (a, i), x_planes[a, i])
+
+        def load_wf(a, b):
+            wf_raw[a, b] = loaded([P, PACK, PASS], F32, "wf%d%d" % (a, b), wf_rows[a, :, :, b * PASS : (b + 1) * PASS])
+
+        def load_ws(b):
+            ws_raw[b] = loaded([P, PACK, N], F32, "ws%d" % b, ws_rows[b])
+
+        def load_skip(h):
+            skip_sb[h] = loaded([P, 4, HALF], F32, "skip%d" % h, skip_rows[:, :, h * HALF : (h + 1) * HALF])
+
+        def load_gain(b):
+            nc.sync.dma_start(out=gain_sb[b][:], in_=gain.rearrange("(b p t) -> b p t", b=2, t=PACK)[b])
+
+        def load_wgt():
+            nc.sync.dma_start(out=wgt_sb[:], in_=wgt)
+
+        def load_offs2():
+            nc.sync.dma_start(offs2_sb[:], offs2)
+
+        def load_table():
+            tab_sb[0] = loaded([P, T], I32, "tab_sb", tab_words[0].rearrange("p t i -> p (t i)").bitcast(I32))
+
+        def load_w4():
+            nc.sync.dma_start(out=w4_raw[:], in_=w4_words[0].bitcast(I32))
+
+        def load_offs():
+            nc.sync.dma_start(offs_sb[:], offs)
+
+        def load_scales(engine, plane, scales):
+            for q in range(4):
+                engine.dma_start(out=plane[32 * q : 32 * q + 4, :], in_=scales[0, 4 * q : 4 * q + 4, :].bitcast(I32))
+
+        nc.vector.memset(tab_plane[:], 0)
+        nc.gpsimd.memset(w4_plane[:], 0)
+        load_scales(nc.scalar, tab_plane, tab_scales)
+        load_scales(nc.gpsimd, w4_plane, w4_scales)
+        load_w4()
+        load_offs()
+        load_wf(0, 0)
+        load_offs2()
+        load_table()
+        load_x(0, 1)
+        load_wgt()
+        load_x(0, 0)
+        load_x(0, 3)
+        load_x(0, 2)
+        load_x(1, 3)
+        load_x(1, 2)
+        load_gain(0)
+        load_gain(1)
+        load_wf(1, 0)
+        load_wf(0, 1)
+        load_x(1, 1)
+        load_x(1, 0)
+        load_ws(0)
+        load_wf(1, 1)
+        load_skip(0)
+        load_skip(1)
+        load_ws(1)
+
+        w4_codes = kept([P, 2 * H], U8, "w4_codes")
+        w4_scale = kept([P, H], U8, "w4_scale")
+        v_codes = kept([P, S], U32, "v_codes")
+        v_scale = kept([P, S], U8, "v_scale")
+        xg_codes = kept([P, 2, S], U32, "xg_codes")
+        xg_scale = kept([P, 2, S], U8, "xg_scale")
+        wf_codes = kept([P, 2, H], U32, "wf_codes")
+        wf_scale = kept([P, 2, H], U8, "wf_scale")
+        ws_codes = kept([P, 2, N], U32, "ws_codes")
+        ws_scale = kept([P, 2, N], U8, "ws_scale")
+        gate = {(h, b): kept([P, PACK, HALF], F32, "gate%d%d" % (h, b)) for h in range(2) for b in range(2)}
+        picked, grouped, filt, hidden, h_codes, h_scale = {}, {}, {}, {}, {}, {}
+
+        def quantize(codes, scale, grouped):
+            nc.vector.quantize_mx(out=codes.bitcast(FP8X4), scales=scale, in_=grouped)
+
+        def by_runs_planes(ap):
+            return ap.rearrange("p t (c i) -> p c t i", i=4)
+
+        def by_runs_grouped(tile):
+            return tile[:].rearrange("p (c i t) -> p c t i", i=4, t=PACK)
+
+        def permute_w4_words():
+            nc.vector.tensor_copy(
+                out=w4_codes[:].bitcast(U16).rearrange("p (b t m) -> p b m t", b=2, t=PACK),
+                in_=w4_raw[:].bitcast(U16).rearrange("p (b m t) -> p b m t", b=2, t=PACK),
+            )
+
+        def permute_w4_scales():
+            nc.vector.tensor_copy(
+                out=w4_scale[:].rearrange("p (b t m) -> p b m t", b=2, t=PACK),
+                in_=w4_plane[:].bitcast(U8).rearrange("p (b m t) -> p b m t", b=2, t=PACK),
+            )
+
+        def list_cols(h):
+            return slice(h * HALF // 16, (h + 1) * HALF // 16)
+
+        def gather_scales(h):
+            cols = slice(h * HALF, (h + 1) * HALF)
+            nc.vector.tensor_copy(v_scale[:, cols], tab_plane[:].bitcast(U8).indirect(offs_sb[:, list_cols(h)]))
+
+        def gather_words(h):
+            cols = slice(h * HALF, (h + 1) * HALF)
+            nc.vector.tensor_copy(v_codes[:, cols], tab_sb[0][:].bitcast(U32).indirect(offs_sb[:, list_cols(h)]))
+
+        def sigmoid_gate(h, b):
+            cols = slice(h * HALF, (h + 1) * HALF)
+            for t in range(PACK):
+                r0 = b * PASS + t * P
+                if t % 2 == 0:
+                    acc = psum.tile([P, 2, HALF], F32, name="acc", tag="acc", bufs=ACC_BUFS)
+                nc.tensor.matmul_mx(
+                    out=acc[:, t % 2, :],
+                    lhsT=w4_codes[:, 2 * r0 : 2 * (r0 + P)].bitcast(FP4X4),
+                    lhsT_scale=w4_scale[:, r0 : r0 + P],
+                    rhs=v_codes[:, cols].bitcast(FP8X4),
+                    rhs_scale=v_scale[:, cols],
+                    start=True,
+                    stop=True,
+                )
+                nc.scalar.activation(out=gate[h, b][:, t, :], in_=acc[:, t % 2, :], func=ACT.Sigmoid)
+
+        def apply_gain(h, b, on_vector):
+            for t in range(PACK):
+                rows = gate[h, b][:, t, :]
+                if on_vector:
+                    nc.vector.tensor_scalar(out=rows, in0=rows, scalar1=gain_sb[b][:, t : t + 1], scalar2=None, op0=MULT)
+                else:
+                    nc.scalar.activation(out=rows, in_=rows, func=ACT.Copy, scale=gain_sb[b][:, t : t + 1])
+
+        def gather_x(a, i, h):
+            if (a, h) not in picked:
+                picked[a, h] = stage.tile([P, PACK, HALF], F32, name="picked", tag="picked", bufs=PICKED_BUFS)
+            nc.vector.tensor_tensor(
+                picked[a, h][:, i, :],
+                x_sb[a, i][:].indirect(offs2_sb[:, list_cols(h)]),
+                wgt_sb[:, h * HALF : (h + 1) * HALF],
+                MULT,
+            )
+
+        def grouped_tile(key, width):
+            if key not in grouped:
+                grouped[key] = stage.tile([P, PACK * width], BF16, name="grouped", tag="grouped", bufs=GROUPED_BUFS, align_bytes=64)
+            return grouped[key]
+
+        def round_copy(target, source, on_vector):
+            copy = nc.vector.tensor_copy if on_vector else nc.scalar.copy
+            copy(out=target, in_=source)
+
+        def round_x(a, j0, on_vector):
+            h, c0 = divmod(j0, HALF)
+            target = by_runs_grouped(grouped_tile(("x", a, j0), CHUNK))
+            round_copy(target, by_runs_planes(picked[a, h][:, :, c0 : c0 + CHUNK]), on_vector)
+
+        def quantize_x(a, j0):
+            quantize(xg_codes[:, a, j0 : j0 + CHUNK], xg_scale[:, a, j0 : j0 + CHUNK], grouped["x", a, j0][:])
+
+        def round_wf(a, b, half, on_vector):
+            m = slice(half * P // 2, (half + 1) * P // 2)
+            target = grouped_tile(("wf", a, b), PASS)[:].rearrange("p (t m i) -> p m i t", t=PACK, i=PACK)
+            source = wf_raw[a, b][:].rearrange("p i (m t) -> p m i t", t=PACK)
+            round_copy(target[:, m], source[:, m], on_vector)
+
+        def quantize_wf(a, b):
+            cols = slice(b * PASS, (b + 1) * PASS)
+            quantize(wf_codes[:, a, cols], wf_scale[:, a, cols], grouped["wf", a, b][:])
+
+        def round_ws(b, half, on_vector):
+            c = slice(half * N // 8, (half + 1) * N // 8)
+            target = by_runs_grouped(grouped_tile(("ws", b), N))
+            round_copy(target[:, c], by_runs_planes(ws_raw[b][:])[:, c], on_vector)
+
+        def quantize_ws(b):
+            quantize(ws_codes[:, b, :], ws_scale[:, b, :], grouped["ws", b][:])
+
+        def tanh_filter(j0, b):
+            cols = slice(j0, j0 + CHUNK)
+            filt[j0, b] = stage.tile([P, PACK, CHUNK], F32, name="filt", tag="filt", bufs=FILT_BUFS)
+            acc = psum.tile([P, PACK, CHUNK], F32, name="acc", tag="acc", bufs=ACC_BUFS)
+            for t0 in range(0, PACK, 2):
+                for t in range(t0, t0 + 2):
+                    r = slice(b * PASS + t * P, b * PASS + (t + 1) * P)
+                    for a in range(2):
+                        nc.tensor.matmul_mx(
+                            out=acc[:, t, :],
+                            lhsT=wf_codes[:, a, r].bitcast(FP8X4),
+                            lhsT_scale=wf_scale[:, a, r],
+                            rhs=xg_codes[:, a, cols].bitcast(FP8X4),
+                            rhs_scale=xg_scale[:, a, cols],
+                            start=(a == 0),
+                            stop=(a == 1),
+                        )
+                nc.scalar.activation(out=filt[j0, b][:, t0 : t0 + 2, :], in_=acc[:, t0 : t0 + 2, :], func=ACT.Tanh)
+
+        def gated_product(j0, b):
+            h, c0 = divmod(j0, HALF)
+            hidden[j0, b] = stage.tile([P, PACK * CHUNK], BF16, name="hidden", tag="hidden", bufs=3, align_bytes=64)
+            nc.vector.tensor_tensor(
+                by_runs_grouped(hidden[j0, b]),
+                by_runs_planes(filt[j0, b][:]),
+                by_runs_planes(gate[h, b][:, :, c0 : c0 + CHUNK]),
+                MULT,
+            )
+
+        def quantize_h(j0, b):
+            h_codes[j0, b] = kept([P, CHUNK], U32, "h_codes%d_%d" % (j0, b))
+            h_scale[j0, b] = kept([P, CHUNK], U8, "h_scale%d_%d" % (j0, b))
+            quantize(h_codes[j0, b][:], h_scale[j0, b][:], hidden[j0, b][:])
+
+        def skip_sum(j0, n0):
+            h, c0 = divmod(j0, HALF)
+            share = psum.tile([P, 2, CHUNK], F32, name="share", tag="share", bufs=8 - 2 * ACC_BUFS)
+            for c in range(n0, n0 + 2):
+                n = slice(c * P, (c + 1) * P)
+                for b in range(2):
+                    nc.tensor.matmul_mx(
+                        out=share[:, c - n0, :],
+                        lhsT=ws_codes[:, b, n].bitcast(FP8X4),
+                        lhsT_scale=ws_scale[:, b, n],
+                        rhs=h_codes[j0, b][:].bitcast(FP8X4),
+                        rhs_scale=h_scale[j0, b][:],
+                        start=(b == 0),
+                        stop=(b == 1),
+                    )
+            rows = skip_sb[h][:, n0 : n0 + 2, c0 : c0 + CHUNK]
+            nc.vector.tensor_tensor(rows, share[:], rows, ADD)
+            nc.sync.dma_start(out=out_rows[:, n0 : n0 + 2, j0 : j0 + CHUNK], in_=rows)
+
+        gather_scales(1)
+        gather_x(1, 0, 0)
+        gather_words(0)
+        gather_x(0, 3, 1)
+        round_wf(1, 1, 1, False)
+        round_ws(1, 0, False)
+        round_wf(0, 0, 1, False)
+        round_wf(1, 0, 1, False)
+        gather_x(1, 3, 0)
+        gather_x(0, 1, 0)
+        gather_x(0, 1, 1)
+        gather_words(1)
+        permute_w4_words()
+        gather_scales(0)
+        gather_x(1, 1, 1)
+        gather_x(1, 1, 0)
+        round_ws(0, 0, True)
+        gather_x(0, 2, 0)
+        permute_w4_scales()
+        sigmoid_gate(1, 0)
+        apply_gain(1, 0, True)
+        gather_x(1, 2, 1)
+        round_ws(0, 1, False)
+        sigmoid_gate(1, 1)
+        apply_gain(1, 1, False)
+        gather_x(1, 2, 0)
+        gather_x(0, 3, 0)
+        round_wf(1, 1, 0, True)
+        round_ws(1, 1, False)
+        round_wf(1, 0, 0, False)
+        gather_x(0, 0, 1)
+        gather_x(0, 2, 1)
+        round_x(1, 256, True)
+        quantize_x(1, 256)
+        sigmoid_gate(0, 0)
+        gather_x(1, 3, 1)
+        sigmoid_gate(0, 1)
+        round_x(1, 0, True)
+        quantize_x(1, 0)
+        gather_x(1, 0, 1)
+        gather_x(0, 0, 0)
+        round_x(1, 512, False)
+        quantize_x(1, 512)
+        round_wf(0, 0, 0, False)
+        quantize_wf(0, 0)
+        round_x(0, 768, False)
+        round_x(0, 256, False)
+        quantize_x(0, 256)
+        round_x(0, 0, True)
+        quantize_wf(1, 1)
+        quantize_x(0, 0)
+        apply_gain(0, 1, False)
+        apply_gain(0, 0, False)
+        quantize_wf(1, 0)
+        round_x(0, 512, True)
+        quantize_x(0, 512)
+        round_wf(0, 1, 1, False)
+        tanh_filter(256, 0)
+        gated_product(256, 0)
+        quantize_h(256, 0)
+        tanh_filter(512, 0)
+        quantize_x(0, 768)
+        tanh_filter(0, 0)
+        round_x(1, 768, False)
+        gated_product(512, 0)
+        quantize_x(1, 768)
+        quantize_h(512, 0)
+        gated_product(0, 0)
+        tanh_filter(768, 0)
+        gated_product(768, 0)
+        quantize_h(768, 0)
+        round_wf(0, 1, 0, False)
+        quantize_ws(1)
+        quantize_wf(0, 1)
+        tanh_filter(512, 1)
+        tanh_filter(256, 1)
+        gated_product(256, 1)
+        tanh_filter(768, 1)
+        tanh_filter(0, 1)
+        gated_product(768, 1)
+        gated_product(0, 1)
+        quantize_h(256, 1)
+        quantize_ws(0)
+        quantize_h(0, 1)
+        quantize_h(768, 1)
+        skip_sum(768, 0)
+        gated_product(512, 1)
+        quantize_h(0, 0)
+        quantize_h(512, 1)
+        skip_sum(512, 0)
+        skip_sum(512, 2)
+        skip_sum(0, 0)
+        skip_sum(768, 2)
+        skip_sum(0, 2)
+        skip_sum(256, 0)
+        skip_sum(256, 2)

@@ -22,8 +22,8 @@ PACK = 4
 PASS = P * PACK
 HALF = 512
 CHUNK = 256
-BIG_BUFS = 12
-ACC_BUFS = 2
+BIG_BUFS = 10
+ACC_BUFS = 4
 PICKED_BUFS = 3
 GROUPED_BUFS = 4
 FILT_BUFS = 2
@@ -72,8 +72,9 @@ def tile_list_vocoder_speaker_gate_skip_kernel(
         def load_ws(b):
             ws_raw[b] = loaded([P, PACK, N], F32, "ws%d" % b, ws_rows[b])
 
-        def load_skip(h):
-            skip_sb[h] = loaded([P, 4, HALF], F32, "skip%d" % h, skip_rows[:, :, h * HALF : (h + 1) * HALF])
+        def load_skip(j0):
+            skip_sb[j0] = keep.tile([P, 4, CHUNK], F32, name="skip%d" % j0, tag="skip%d" % j0)
+            nc.sync.dma_start(out=skip_sb[j0][:], in_=skip_rows[:, :, j0 : j0 + CHUNK])
 
         def load_gain(b):
             nc.sync.dma_start(out=gain_sb[b][:], in_=gain.rearrange("(b p t) -> b p t", b=2, t=PACK)[b])
@@ -98,32 +99,34 @@ def tile_list_vocoder_speaker_gate_skip_kernel(
                 engine.dma_start(out=plane[32 * q : 32 * q + 4, :], in_=scales[0, 4 * q : 4 * q + 4, :].bitcast(I32))
 
         nc.vector.memset(tab_plane[:], 0)
-        nc.gpsimd.memset(w4_plane[:], 0)
-        load_scales(nc.scalar, tab_plane, tab_scales)
-        load_scales(nc.gpsimd, w4_plane, w4_scales)
-        load_w4()
+        nc.vector.memset(w4_plane[:], 0)
+        load_scales(nc.sync, tab_plane, tab_scales)
+        load_table()
         load_offs()
         load_wf(0, 0)
         load_offs2()
-        load_table()
-        load_x(0, 1)
-        load_wgt()
+        load_w4()
         load_x(0, 0)
-        load_x(0, 3)
-        load_x(0, 2)
+        load_scales(nc.sync, w4_plane, w4_scales)
+        load_wgt()
         load_x(1, 3)
-        load_x(1, 2)
-        load_gain(0)
         load_gain(1)
+        load_x(0, 3)
+        load_gain(0)
+        load_x(1, 1)
+        load_x(1, 2)
+        load_x(1, 0)
+        load_x(0, 2)
+        load_x(0, 1)
+        load_wf(1, 1)
         load_wf(1, 0)
         load_wf(0, 1)
-        load_x(1, 1)
-        load_x(1, 0)
         load_ws(0)
-        load_wf(1, 1)
         load_skip(0)
-        load_skip(1)
+        load_skip(256)
         load_ws(1)
+        load_skip(768)
+        load_skip(512)
 
         w4_codes = kept([P, 2 * H], U8, "w4_codes")
         w4_scale = kept([P, H], U8, "w4_scale")
@@ -174,10 +177,9 @@ def tile_list_vocoder_speaker_gate_skip_kernel(
             cols = slice(h * HALF, (h + 1) * HALF)
             for t in range(PACK):
                 r0 = b * PASS + t * P
-                if t % 2 == 0:
-                    acc = psum.tile([P, 2, HALF], F32, name="acc", tag="acc", bufs=ACC_BUFS)
+                acc = psum.tile([P, HALF], F32, name="acc", tag="acc", bufs=ACC_BUFS)
                 nc.tensor.matmul_mx(
-                    out=acc[:, t % 2, :],
+                    out=acc[:],
                     lhsT=w4_codes[:, 2 * r0 : 2 * (r0 + P)].bitcast(FP4X4),
                     lhsT_scale=w4_scale[:, r0 : r0 + P],
                     rhs=v_codes[:, cols].bitcast(FP8X4),
@@ -185,7 +187,7 @@ def tile_list_vocoder_speaker_gate_skip_kernel(
                     start=True,
                     stop=True,
                 )
-                nc.scalar.activation(out=gate[h, b][:, t, :], in_=acc[:, t % 2, :], func=ACT.Sigmoid)
+                nc.scalar.activation(out=gate[h, b][:, t, :], in_=acc[:], func=ACT.Sigmoid)
 
         def apply_gain(h, b, on_vector):
             for t in range(PACK):
@@ -243,13 +245,13 @@ def tile_list_vocoder_speaker_gate_skip_kernel(
         def tanh_filter(j0, b):
             cols = slice(j0, j0 + CHUNK)
             filt[j0, b] = stage.tile([P, PACK, CHUNK], F32, name="filt", tag="filt", bufs=FILT_BUFS)
-            acc = psum.tile([P, PACK, CHUNK], F32, name="acc", tag="acc", bufs=ACC_BUFS)
             for t0 in range(0, PACK, 2):
+                acc = psum.tile([P, 2, CHUNK], F32, name="acc", tag="acc", bufs=ACC_BUFS)
                 for t in range(t0, t0 + 2):
                     r = slice(b * PASS + t * P, b * PASS + (t + 1) * P)
                     for a in range(2):
                         nc.tensor.matmul_mx(
-                            out=acc[:, t, :],
+                            out=acc[:, t - t0, :],
                             lhsT=wf_codes[:, a, r].bitcast(FP8X4),
                             lhsT_scale=wf_scale[:, a, r],
                             rhs=xg_codes[:, a, cols].bitcast(FP8X4),
@@ -257,7 +259,7 @@ def tile_list_vocoder_speaker_gate_skip_kernel(
                             start=(a == 0),
                             stop=(a == 1),
                         )
-                nc.scalar.activation(out=filt[j0, b][:, t0 : t0 + 2, :], in_=acc[:, t0 : t0 + 2, :], func=ACT.Tanh)
+                nc.scalar.activation(out=filt[j0, b][:, t0 : t0 + 2, :], in_=acc[:], func=ACT.Tanh)
 
         def gated_product(j0, b):
             h, c0 = divmod(j0, HALF)
@@ -275,8 +277,7 @@ def tile_list_vocoder_speaker_gate_skip_kernel(
             quantize(h_codes[j0, b][:], h_scale[j0, b][:], hidden[j0, b][:])
 
         def skip_sum(j0, n0):
-            h, c0 = divmod(j0, HALF)
-            share = psum.tile([P, 2, CHUNK], F32, name="share", tag="share", bufs=8 - 2 * ACC_BUFS)
+            share = psum.tile([P, 2, CHUNK], F32, name="share", tag="share", bufs=8 - ACC_BUFS)
             for c in range(n0, n0 + 2):
                 n = slice(c * P, (c + 1) * P)
                 for b in range(2):
@@ -289,103 +290,103 @@ def tile_list_vocoder_speaker_gate_skip_kernel(
                         start=(b == 0),
                         stop=(b == 1),
                     )
-            rows = skip_sb[h][:, n0 : n0 + 2, c0 : c0 + CHUNK]
+            rows = skip_sb[j0][:, n0 : n0 + 2, :]
             nc.vector.tensor_tensor(rows, share[:], rows, ADD)
             nc.sync.dma_start(out=out_rows[:, n0 : n0 + 2, j0 : j0 + CHUNK], in_=rows)
 
-        gather_scales(1)
-        gather_x(1, 0, 0)
-        gather_words(0)
+        round_wf(0, 0, 0, False)
+        gather_x(0, 0, 0)
         gather_x(0, 3, 1)
         round_wf(1, 1, 1, False)
-        round_ws(1, 0, False)
-        round_wf(0, 0, 1, False)
+        gather_x(1, 1, 0)
+        gather_x(0, 2, 0)
+        gather_x(0, 1, 0)
+        gather_x(1, 0, 0)
+        gather_x(1, 0, 1)
+        gather_x(0, 3, 0)
+        round_x(0, 0, False)
+        gather_x(0, 1, 1)
+        gather_x(1, 2, 0)
+        round_wf(1, 1, 0, True)
+        gather_x(0, 2, 1)
+        gather_x(0, 0, 1)
+        round_x(0, 512, True)
+        permute_w4_scales()
+        round_x(0, 256, False)
+        gather_x(1, 1, 1)
+        permute_w4_words()
+        gather_words(1)
         round_wf(1, 0, 1, False)
         gather_x(1, 3, 0)
-        gather_x(0, 1, 0)
-        gather_x(0, 1, 1)
-        gather_words(1)
-        permute_w4_words()
-        gather_scales(0)
-        gather_x(1, 1, 1)
-        gather_x(1, 1, 0)
-        round_ws(0, 0, True)
-        gather_x(0, 2, 0)
-        permute_w4_scales()
-        sigmoid_gate(1, 0)
-        apply_gain(1, 0, True)
         gather_x(1, 2, 1)
-        round_ws(0, 1, False)
-        sigmoid_gate(1, 1)
-        apply_gain(1, 1, False)
-        gather_x(1, 2, 0)
-        gather_x(0, 3, 0)
-        round_wf(1, 1, 0, True)
-        round_ws(1, 1, False)
-        round_wf(1, 0, 0, False)
-        gather_x(0, 0, 1)
-        gather_x(0, 2, 1)
-        round_x(1, 256, True)
-        quantize_x(1, 256)
-        sigmoid_gate(0, 0)
-        gather_x(1, 3, 1)
-        sigmoid_gate(0, 1)
-        round_x(1, 0, True)
-        quantize_x(1, 0)
-        gather_x(1, 0, 1)
-        gather_x(0, 0, 0)
-        round_x(1, 512, False)
-        quantize_x(1, 512)
-        round_wf(0, 0, 0, False)
-        quantize_wf(0, 0)
-        round_x(0, 768, False)
-        round_x(0, 256, False)
-        quantize_x(0, 256)
-        round_x(0, 0, True)
-        quantize_wf(1, 1)
-        quantize_x(0, 0)
-        apply_gain(0, 1, False)
-        apply_gain(0, 0, False)
-        quantize_wf(1, 0)
-        round_x(0, 512, True)
         quantize_x(0, 512)
-        round_wf(0, 1, 1, False)
+        round_x(1, 0, False)
+        quantize_x(1, 0)
+        round_x(0, 768, False)
+        round_x(1, 256, False)
+        quantize_x(0, 0)
+        gather_x(1, 3, 1)
+        quantize_x(1, 256)
+        round_x(1, 768, True)
+        round_wf(0, 1, 0, True)
+        round_ws(0, 0, False)
+        gather_words(0)
+        gather_scales(0)
+        sigmoid_gate(0, 0)
+        round_wf(1, 0, 0, True)
+        apply_gain(0, 0, True)
+        quantize_x(0, 768)
+        sigmoid_gate(0, 1)
+        gather_scales(1)
+        sigmoid_gate(1, 0)
+        round_wf(0, 0, 1, False)
+        quantize_wf(0, 0)
+        sigmoid_gate(1, 1)
+        quantize_x(0, 256)
+        apply_gain(1, 1, False)
+        round_x(1, 512, True)
+        quantize_wf(1, 0)
         tanh_filter(256, 0)
         gated_product(256, 0)
         quantize_h(256, 0)
-        tanh_filter(512, 0)
-        quantize_x(0, 768)
+        quantize_x(1, 512)
+        round_wf(0, 1, 1, True)
+        quantize_wf(1, 1)
+        apply_gain(1, 0, False)
         tanh_filter(0, 0)
-        round_x(1, 768, False)
-        gated_product(512, 0)
         quantize_x(1, 768)
-        quantize_h(512, 0)
-        gated_product(0, 0)
         tanh_filter(768, 0)
+        round_ws(0, 1, False)
+        tanh_filter(512, 0)
+        gated_product(0, 0)
+        quantize_ws(0)
+        apply_gain(0, 1, False)
         gated_product(768, 0)
         quantize_h(768, 0)
-        round_wf(0, 1, 0, False)
-        quantize_ws(1)
         quantize_wf(0, 1)
-        tanh_filter(512, 1)
-        tanh_filter(256, 1)
-        gated_product(256, 1)
-        tanh_filter(768, 1)
+        round_ws(1, 0, False)
         tanh_filter(0, 1)
-        gated_product(768, 1)
+        gated_product(512, 0)
+        round_ws(1, 1, False)
+        quantize_ws(1)
         gated_product(0, 1)
-        quantize_h(256, 1)
-        quantize_ws(0)
         quantize_h(0, 1)
-        quantize_h(768, 1)
-        skip_sum(768, 0)
-        gated_product(512, 1)
         quantize_h(0, 0)
+        tanh_filter(512, 1)
+        gated_product(512, 1)
+        tanh_filter(256, 1)
         quantize_h(512, 1)
-        skip_sum(512, 0)
-        skip_sum(512, 2)
+        gated_product(256, 1)
+        quantize_h(256, 1)
+        tanh_filter(768, 1)
         skip_sum(0, 0)
-        skip_sum(768, 2)
-        skip_sum(0, 2)
-        skip_sum(256, 0)
         skip_sum(256, 2)
+        quantize_h(512, 0)
+        gated_product(768, 1)
+        quantize_h(768, 1)
+        skip_sum(256, 0)
+        skip_sum(0, 2)
+        skip_sum(512, 2)
+        skip_sum(768, 2)
+        skip_sum(768, 0)
+        skip_sum(512, 0)

@@ -145,10 +145,10 @@ def tile_list_vocoder_speaker_gate_skip_kernel(
             nc.vector.quantize_mx(out=codes.bitcast(FP8X4), scales=scale, in_=grouped)
 
         def by_runs_planes(ap):
-            return ap.rearrange("p t (c i) -> p c t i", i=4)
+            return ap.rearrange("p t (c i) -> p c t i", i=2)
 
         def by_runs_grouped(tile):
-            return tile[:].rearrange("p (c i t) -> p c t i", i=4, t=PACK)
+            return tile[:].rearrange("p (c i t) -> p c t i", i=2, t=PACK)
 
         def permute_w4_words():
             nc.vector.tensor_copy(
@@ -235,7 +235,7 @@ def tile_list_vocoder_speaker_gate_skip_kernel(
             quantize(wf_codes[:, a, cols], wf_scale[:, a, cols], grouped["wf", a, b][:])
 
         def round_ws(b, half, on_vector):
-            c = slice(half * N // 8, (half + 1) * N // 8)
+            c = slice(half * N // 4, (half + 1) * N // 4)
             target = by_runs_grouped(grouped_tile(("ws", b), N))
             round_copy(target[:, c], by_runs_planes(ws_raw[b][:])[:, c], on_vector)
 

@@ -22,11 +22,7 @@ PACK = 4
 PASS = P * PACK
 HALF = 512
 CHUNK = 256
-BIG_BUFS = 10
 ACC_BUFS = 4
-PICKED_BUFS = 3
-GROUPED_BUFS = 4
-FILT_BUFS = 2
 
 
 def tile_list_vocoder_speaker_gate_skip_kernel(
@@ -35,25 +31,28 @@ def tile_list_vocoder_speaker_gate_skip_kernel(
     nc = tc.nc
     with ExitStack() as ctx:
         keep = ctx.enter_context(tc.tile_pool(name="keep", bufs=1))
-        big = ctx.enter_context(tc.tile_pool(name="big", bufs=BIG_BUFS))
+        slots = ctx.enter_context(tc.tile_pool(name="slots", bufs=1))
         stage = ctx.enter_context(tc.tile_pool(name="stage", bufs=3))
         psum = ctx.enter_context(tc.psum_pool(name="psum", bufs=1))
 
         def kept(shape, dtype, name):
             return keep.tile(shape, dtype, name=name, align_bytes=64)
 
-        def loaded(shape, dtype, name, source):
-            tile = big.tile(shape, dtype, name=name, tag="big", align_bytes=64)
+        def in_slot(slot, shape, dtype, name):
+            return slots.tile(shape, dtype, name=name, tag=slot, align_bytes=64)
+
+        def loaded(slot, shape, dtype, name, source):
+            tile = in_slot(slot, shape, dtype, name)
             nc.sync.dma_start(out=tile[:], in_=source)
             return tile
 
         offs_sb = kept([P, S // 16], U16, "offs_sb")
         offs2_sb = kept([P, S // 16], U16, "offs2_sb")
         tab_plane = kept([P, T // 4], I32, "tab_plane")
-        w4_plane = kept([P, H // 4], I32, "w4_plane")
+        w4_plane = in_slot("w4_plane", [P, H // 4], I32, "w4_plane")
         w4_raw = kept([P, H // 2], I32, "w4_raw")
         wgt_sb = kept([P, S], F32, "wgt_sb")
-        gain_sb = [kept([P, PACK], F32, "gain%d" % b) for b in range(2)]
+        gain_sb = kept([P, 2, PACK], F32, "gain_sb")
 
         x_planes = xT.rearrange("(a p i) t -> a i p t", a=2, i=PACK)
         wf_rows = wf.rearrange("(a p i) r -> a p i r", a=2, i=PACK)
@@ -61,94 +60,42 @@ def tile_list_vocoder_speaker_gate_skip_kernel(
         skip_rows = skip.rearrange("(c p) j -> p c j", p=P)
         out_rows = out.rearrange("(c p) j -> p c j", p=P)
 
-        tab_sb, x_sb, wf_raw, ws_raw, skip_sb = {}, {}, {}, {}, {}
+        x_sb, wf_raw, ws_raw, skip_sb = {}, {}, {}, {}
 
         def load_x(a, i):
-            x_sb[a, i] = loaded([P, T], F32, "x%d%d" % (a, i), x_planes[a, i])
+            x_sb[a, i] = loaded("x%d%d" % (a, i), [P, T], F32, "x%d%d" % (a, i), x_planes[a, i])
 
         def load_wf(a, b):
-            wf_raw[a, b] = loaded([P, PACK, PASS], F32, "wf%d%d" % (a, b), wf_rows[a, :, :, b * PASS : (b + 1) * PASS])
+            wf_raw[a, b] = loaded("wf%d%d" % (a, b), [P, PACK, PASS], F32, "wf%d%d" % (a, b), wf_rows[a, :, :, b * PASS : (b + 1) * PASS])
 
         def load_ws(b):
-            ws_raw[b] = loaded([P, PACK, N], F32, "ws%d" % b, ws_rows[b])
+            ws_raw[b] = loaded("x0%d" % b, [P, PACK, N], F32, "ws%d" % b, ws_rows[b])
 
-        def load_skip(j0):
-            skip_sb[j0] = keep.tile([P, 4, CHUNK], F32, name="skip%d" % j0, tag="skip%d" % j0)
-            nc.sync.dma_start(out=skip_sb[j0][:], in_=skip_rows[:, :, j0 : j0 + CHUNK])
+        def load_skip(h):
+            skip_sb[h] = loaded("x0%d" % (2 + h), [P, 4, HALF], F32, "skip%d" % h, skip_rows[:, :, h * HALF : (h + 1) * HALF])
 
-        def load_gain(b):
-            nc.sync.dma_start(out=gain_sb[b][:], in_=gain.rearrange("(b p t) -> b p t", b=2, t=PACK)[b])
-
-        def load_wgt():
-            nc.sync.dma_start(out=wgt_sb[:], in_=wgt)
-
-        def load_offs2():
-            nc.sync.dma_start(offs2_sb[:], offs2)
-
-        def load_table():
-            tab_sb[0] = loaded([P, T], I32, "tab_sb", tab_words[0].rearrange("p t i -> p (t i)").bitcast(I32))
-
-        def load_w4():
-            nc.sync.dma_start(out=w4_raw[:], in_=w4_words[0].bitcast(I32))
-
-        def load_offs():
-            nc.sync.dma_start(offs_sb[:], offs)
-
-        def load_scales(engine, plane, scales):
+        def load_scales(plane, scales):
             for q in range(4):
-                engine.dma_start(out=plane[32 * q : 32 * q + 4, :], in_=scales[0, 4 * q : 4 * q + 4, :].bitcast(I32))
-
-        nc.vector.memset(tab_plane[:], 0)
-        nc.vector.memset(w4_plane[:], 0)
-        load_scales(nc.sync, tab_plane, tab_scales)
-        load_table()
-        load_offs()
-        load_wf(0, 0)
-        load_offs2()
-        load_w4()
-        load_x(0, 0)
-        load_scales(nc.sync, w4_plane, w4_scales)
-        load_wgt()
-        load_x(1, 3)
-        load_gain(1)
-        load_x(0, 3)
-        load_gain(0)
-        load_x(1, 1)
-        load_x(1, 2)
-        load_x(1, 0)
-        load_x(0, 2)
-        load_x(0, 1)
-        load_wf(1, 1)
-        load_wf(1, 0)
-        load_wf(0, 1)
-        load_ws(0)
-        load_skip(0)
-        load_skip(256)
-        load_ws(1)
-        load_skip(768)
-        load_skip(512)
+                nc.sync.dma_start(out=plane[32 * q : 32 * q + 4, :], in_=scales[0, 4 * q : 4 * q + 4, :].bitcast(I32))
 
         w4_codes = kept([P, 2 * H], U8, "w4_codes")
         w4_scale = kept([P, H], U8, "w4_scale")
-        v_codes = kept([P, S], U32, "v_codes")
+        v_codes = {}
         v_scale = kept([P, S], U8, "v_scale")
-        xg_codes = kept([P, 2, S], U32, "xg_codes")
         xg_scale = kept([P, 2, S], U8, "xg_scale")
-        wf_codes = kept([P, 2, H], U32, "wf_codes")
         wf_scale = kept([P, 2, H], U8, "wf_scale")
         ws_codes = kept([P, 2, N], U32, "ws_codes")
         ws_scale = kept([P, 2, N], U8, "ws_scale")
-        gate = {(h, b): kept([P, PACK, HALF], F32, "gate%d%d" % (h, b)) for h in range(2) for b in range(2)}
-        picked, grouped, filt, hidden, h_codes, h_scale = {}, {}, {}, {}, {}, {}
+        sig, gate, picked, grouped, filt, hidden, h_codes, h_scale, xg_codes, wf_codes = {}, {}, {}, {}, {}, {}, {}, {}, {}, {}
 
-        def quantize(codes, scale, grouped):
-            nc.vector.quantize_mx(out=codes.bitcast(FP8X4), scales=scale, in_=grouped)
+        def quantize(codes, scale, values):
+            nc.vector.quantize_mx(out=codes.bitcast(FP8X4), scales=scale, in_=values)
 
         def by_runs_planes(ap):
             return ap.rearrange("p t (c i) -> p c t i", i=2)
 
-        def by_runs_grouped(tile):
-            return tile[:].rearrange("p (c i t) -> p c t i", i=2, t=PACK)
+        def by_runs_grouped(ap):
+            return ap.rearrange("p (c i t) -> p c t i", i=2, t=PACK)
 
         def permute_w4_words():
             nc.vector.tensor_copy(
@@ -162,19 +109,20 @@ def tile_list_vocoder_speaker_gate_skip_kernel(
                 in_=w4_plane[:].bitcast(U8).rearrange("p (b m t) -> p b m t", b=2, t=PACK),
             )
 
-        def list_cols(h):
-            return slice(h * HALF // 16, (h + 1) * HALF // 16)
+        def list_cols(j0, width):
+            return slice(j0 // 16, (j0 + width) // 16)
 
         def gather_scales(h):
             cols = slice(h * HALF, (h + 1) * HALF)
-            nc.vector.tensor_copy(v_scale[:, cols], tab_plane[:].bitcast(U8).indirect(offs_sb[:, list_cols(h)]))
+            nc.vector.tensor_copy(v_scale[:, cols], tab_plane[:].bitcast(U8).indirect(offs_sb[:, list_cols(h * HALF, HALF)]))
 
         def gather_words(h):
-            cols = slice(h * HALF, (h + 1) * HALF)
-            nc.vector.tensor_copy(v_codes[:, cols], tab_sb[0][:].bitcast(U32).indirect(offs_sb[:, list_cols(h)]))
+            v_codes[h] = in_slot("w4_plane" if h else "v_codes0", [P, HALF], U32, "v_codes%d" % h)
+            nc.vector.tensor_copy(v_codes[h][:], tab_sb[:].bitcast(U32).indirect(offs_sb[:, list_cols(h * HALF, HALF)]))
 
         def sigmoid_gate(h, b):
             cols = slice(h * HALF, (h + 1) * HALF)
+            sig[h, b] = kept([P, PACK, HALF], F32, "sig%d%d" % (h, b))
             for t in range(PACK):
                 r0 = b * PASS + t * P
                 acc = psum.tile([P, HALF], F32, name="acc", tag="acc", bufs=ACC_BUFS)
@@ -182,101 +130,103 @@ def tile_list_vocoder_speaker_gate_skip_kernel(
                     out=acc[:],
                     lhsT=w4_codes[:, 2 * r0 : 2 * (r0 + P)].bitcast(FP4X4),
                     lhsT_scale=w4_scale[:, r0 : r0 + P],
-                    rhs=v_codes[:, cols].bitcast(FP8X4),
+                    rhs=v_codes[h][:].bitcast(FP8X4),
                     rhs_scale=v_scale[:, cols],
                     start=True,
                     stop=True,
                 )
-                nc.scalar.activation(out=gate[h, b][:, t, :], in_=acc[:], func=ACT.Sigmoid)
+                nc.scalar.activation(out=sig[h, b][:, t, :], in_=acc[:], func=ACT.Sigmoid)
 
-        def apply_gain(h, b, on_vector):
+        def apply_gain(h, b, slot):
+            gate[h, b] = in_slot(slot, [P, PACK, HALF], F32, "gate%d%d" % (h, b)) if slot else sig[h, b]
             for t in range(PACK):
-                rows = gate[h, b][:, t, :]
-                if on_vector:
-                    nc.vector.tensor_scalar(out=rows, in0=rows, scalar1=gain_sb[b][:, t : t + 1], scalar2=None, op0=MULT)
-                else:
-                    nc.scalar.activation(out=rows, in_=rows, func=ACT.Copy, scale=gain_sb[b][:, t : t + 1])
+                nc.scalar.activation(out=gate[h, b][:, t, :], in_=sig[h, b][:, t, :], func=ACT.Copy, scale=gain_sb[:, b, t : t + 1])
 
-        def gather_x(a, i, h):
-            if (a, h) not in picked:
-                picked[a, h] = stage.tile([P, PACK, HALF], F32, name="picked", tag="picked", bufs=PICKED_BUFS)
+        def gather_x(a, i, j0, width):
+            if a not in picked:
+                picked[a] = in_slot("picked%d" % a, [P, PACK, S], F32, "picked%d" % a)
             nc.vector.tensor_tensor(
-                picked[a, h][:, i, :],
-                x_sb[a, i][:].indirect(offs2_sb[:, list_cols(h)]),
-                wgt_sb[:, h * HALF : (h + 1) * HALF],
+                picked[a][:, i, j0 : j0 + width],
+                x_sb[a, i][:].indirect(offs2_sb[:, list_cols(j0, width)]),
+                wgt_sb[:, j0 : j0 + width],
                 MULT,
             )
-
-        def grouped_tile(key, width):
-            if key not in grouped:
-                grouped[key] = stage.tile([P, PACK * width], BF16, name="grouped", tag="grouped", bufs=GROUPED_BUFS, align_bytes=64)
-            return grouped[key]
 
         def round_copy(target, source, on_vector):
             copy = nc.vector.tensor_copy if on_vector else nc.scalar.copy
             copy(out=target, in_=source)
 
-        def round_x(a, j0, on_vector):
-            h, c0 = divmod(j0, HALF)
-            target = by_runs_grouped(grouped_tile(("x", a, j0), CHUNK))
-            round_copy(target, by_runs_planes(picked[a, h][:, :, c0 : c0 + CHUNK]), on_vector)
+        def staged(width):
+            return stage.tile([P, PACK * width], BF16, name="grouped", tag="grouped", bufs=3, align_bytes=64)
 
-        def quantize_x(a, j0):
-            quantize(xg_codes[:, a, j0 : j0 + CHUNK], xg_scale[:, a, j0 : j0 + CHUNK], grouped["x", a, j0][:])
+        def round_x(a, j0, width, target):
+            round_copy(by_runs_grouped(target), by_runs_planes(picked[a][:, :, j0 : j0 + width]), False)
 
-        def round_wf(a, b, half, on_vector):
-            m = slice(half * P // 2, (half + 1) * P // 2)
-            target = grouped_tile(("wf", a, b), PASS)[:].rearrange("p (t m i) -> p m i t", t=PACK, i=PACK)
-            source = wf_raw[a, b][:].rearrange("p i (m t) -> p m i t", t=PACK)
-            round_copy(target[:, m], source[:, m], on_vector)
+        def round_x1(j0, slot=None):
+            if slot:
+                grouped["x", j0] = in_slot(slot, [P, PACK * CHUNK], BF16, "gx1_held")
+            else:
+                grouped["x", j0] = stage.tile([P, PACK * CHUNK], BF16, name="gx1", tag="gx1", bufs=3, align_bytes=64)
+            round_x(1, j0, CHUNK, grouped["x", j0][:])
 
-        def quantize_wf(a, b):
-            cols = slice(b * PASS, (b + 1) * PASS)
-            quantize(wf_codes[:, a, cols], wf_scale[:, a, cols], grouped["wf", a, b][:])
+        def quantize_x1(j0, slot):
+            xg_codes[1, j0] = in_slot(slot, [P, CHUNK], U32, "xg1_%d" % j0)[:]
+            quantize(xg_codes[1, j0], xg_scale[:, 1, j0 : j0 + CHUNK], grouped["x", j0][:])
 
-        def round_ws(b, half, on_vector):
-            c = slice(half * N // 4, (half + 1) * N // 4)
-            target = by_runs_grouped(grouped_tile(("ws", b), N))
-            round_copy(target[:, c], by_runs_planes(ws_raw[b][:])[:, c], on_vector)
+        def round_wf(a, b, on_vector):
+            grouped["wf", a, b] = staged(PASS)
+            target = grouped["wf", a, b][:].rearrange("p (t m i) -> p m i t", t=PACK, i=PACK)
+            round_copy(target, wf_raw[a, b][:].rearrange("p i (m t) -> p m i t", t=PACK), on_vector)
+
+        def quantize_wf(a, b, codes):
+            wf_codes[a, b] = codes
+            quantize(codes, wf_scale[:, a, b * PASS : (b + 1) * PASS], grouped["wf", a, b][:])
+
+        def round_ws(b, on_vector):
+            grouped["ws", b] = staged(N)
+            round_copy(by_runs_grouped(grouped["ws", b][:]), by_runs_planes(ws_raw[b][:]), on_vector)
 
         def quantize_ws(b):
             quantize(ws_codes[:, b, :], ws_scale[:, b, :], grouped["ws", b][:])
 
         def tanh_filter(j0, b):
             cols = slice(j0, j0 + CHUNK)
-            filt[j0, b] = stage.tile([P, PACK, CHUNK], F32, name="filt", tag="filt", bufs=FILT_BUFS)
+            filt[j0, b] = stage.tile([P, PACK, CHUNK], F32, name="filt", tag="filt", bufs=3)
             for t0 in range(0, PACK, 2):
                 acc = psum.tile([P, 2, CHUNK], F32, name="acc", tag="acc", bufs=ACC_BUFS)
                 for t in range(t0, t0 + 2):
-                    r = slice(b * PASS + t * P, b * PASS + (t + 1) * P)
                     for a in range(2):
                         nc.tensor.matmul_mx(
                             out=acc[:, t - t0, :],
-                            lhsT=wf_codes[:, a, r].bitcast(FP8X4),
-                            lhsT_scale=wf_scale[:, a, r],
-                            rhs=xg_codes[:, a, cols].bitcast(FP8X4),
+                            lhsT=wf_codes[a, b][:, t * P : (t + 1) * P].bitcast(FP8X4),
+                            lhsT_scale=wf_scale[:, a, b * PASS + t * P : b * PASS + (t + 1) * P],
+                            rhs=xg_codes[a, j0].bitcast(FP8X4),
                             rhs_scale=xg_scale[:, a, cols],
                             start=(a == 0),
                             stop=(a == 1),
                         )
                 nc.scalar.activation(out=filt[j0, b][:, t0 : t0 + 2, :], in_=acc[:], func=ACT.Tanh)
 
-        def gated_product(j0, b):
+        def gated_product(j0, b, slot=None):
             h, c0 = divmod(j0, HALF)
-            hidden[j0, b] = stage.tile([P, PACK * CHUNK], BF16, name="hidden", tag="hidden", bufs=3, align_bytes=64)
+            if slot:
+                hidden[j0, b] = in_slot(slot, [P, PACK * CHUNK], BF16, "hidden_first")
+            else:
+                hidden[j0, b] = stage.tile([P, PACK * CHUNK], BF16, name="hidden", tag="hidden", bufs=3, align_bytes=64)
             nc.vector.tensor_tensor(
-                by_runs_grouped(hidden[j0, b]),
+                by_runs_grouped(hidden[j0, b][:]),
                 by_runs_planes(filt[j0, b][:]),
                 by_runs_planes(gate[h, b][:, :, c0 : c0 + CHUNK]),
                 MULT,
             )
 
         def quantize_h(j0, b):
-            h_codes[j0, b] = kept([P, CHUNK], U32, "h_codes%d_%d" % (j0, b))
+            h_codes[j0, b] = h_all[:, b, j0 : j0 + CHUNK]
             h_scale[j0, b] = kept([P, CHUNK], U8, "h_scale%d_%d" % (j0, b))
-            quantize(h_codes[j0, b][:], h_scale[j0, b][:], hidden[j0, b][:])
+            quantize(h_codes[j0, b], h_scale[j0, b][:], hidden[j0, b][:])
 
         def skip_sum(j0, n0):
+            h, c0 = divmod(j0, HALF)
             share = psum.tile([P, 2, CHUNK], F32, name="share", tag="share", bufs=8 - ACC_BUFS)
             for c in range(n0, n0 + 2):
                 n = slice(c * P, (c + 1) * P)
@@ -285,108 +235,120 @@ def tile_list_vocoder_speaker_gate_skip_kernel(
                         out=share[:, c - n0, :],
                         lhsT=ws_codes[:, b, n].bitcast(FP8X4),
                         lhsT_scale=ws_scale[:, b, n],
-                        rhs=h_codes[j0, b][:].bitcast(FP8X4),
+                        rhs=h_codes[j0, b].bitcast(FP8X4),
                         rhs_scale=h_scale[j0, b][:],
                         start=(b == 0),
                         stop=(b == 1),
                     )
-            rows = skip_sb[j0][:, n0 : n0 + 2, :]
+            rows = skip_sb[h][:, n0 : n0 + 2, c0 : c0 + CHUNK]
             nc.vector.tensor_tensor(rows, share[:], rows, ADD)
             nc.sync.dma_start(out=out_rows[:, n0 : n0 + 2, j0 : j0 + CHUNK], in_=rows)
 
-        round_wf(0, 0, 0, False)
-        gather_x(0, 0, 0)
-        gather_x(0, 3, 1)
-        round_wf(1, 1, 1, False)
-        gather_x(1, 1, 0)
-        gather_x(0, 2, 0)
-        gather_x(0, 1, 0)
-        gather_x(1, 0, 0)
-        gather_x(1, 0, 1)
-        gather_x(0, 3, 0)
-        round_x(0, 0, False)
-        gather_x(0, 1, 1)
-        gather_x(1, 2, 0)
-        round_wf(1, 1, 0, True)
-        gather_x(0, 2, 1)
-        gather_x(0, 0, 1)
-        round_x(0, 512, True)
-        permute_w4_scales()
-        round_x(0, 256, False)
-        gather_x(1, 1, 1)
+        nc.vector.memset(tab_plane[:], 0)
+        nc.vector.memset(w4_plane[:], 0)
+        nc.sync.dma_start(offs_sb[:], offs)
+        nc.sync.dma_start(offs2_sb[:], offs2)
+        nc.sync.dma_start(out=w4_raw[:], in_=w4_words[0].bitcast(I32))
+        load_scales(tab_plane, tab_scales)
+        tab_sb = loaded("tab", [P, T], I32, "tab_sb", tab_words[0].rearrange("p t i -> p (t i)").bitcast(I32))
+        load_scales(w4_plane, w4_scales)
+        load_x(0, 0)
+        nc.sync.dma_start(out=wgt_sb[:], in_=wgt)
+        load_x(0, 1)
+        nc.sync.dma_start(out=gain_sb[:], in_=gain.rearrange("(b p t) -> p b t", b=2, t=PACK))
+        load_x(0, 2)
+        load_x(0, 3)
+        load_wf(0, 0)
+        load_x(1, 0)
+        load_x(1, 1)
+        load_wf(1, 0)
+        load_x(1, 2)
+        load_x(1, 3)
+        load_wf(0, 1)
+        load_wf(1, 1)
+
         permute_w4_words()
-        gather_words(1)
-        round_wf(1, 0, 1, False)
-        gather_x(1, 3, 0)
-        gather_x(1, 2, 1)
-        quantize_x(0, 512)
-        round_x(1, 0, False)
-        quantize_x(1, 0)
-        round_x(0, 768, False)
-        round_x(1, 256, False)
-        quantize_x(0, 0)
-        gather_x(1, 3, 1)
-        quantize_x(1, 256)
-        round_x(1, 768, True)
-        round_wf(0, 1, 0, True)
-        round_ws(0, 0, False)
-        gather_words(0)
         gather_scales(0)
-        sigmoid_gate(0, 0)
-        round_wf(1, 0, 0, True)
-        apply_gain(0, 0, True)
-        quantize_x(0, 768)
-        sigmoid_gate(0, 1)
         gather_scales(1)
-        sigmoid_gate(1, 0)
-        round_wf(0, 0, 1, False)
-        quantize_wf(0, 0)
-        sigmoid_gate(1, 1)
-        quantize_x(0, 256)
-        apply_gain(1, 1, False)
-        round_x(1, 512, True)
-        quantize_wf(1, 0)
-        tanh_filter(256, 0)
-        gated_product(256, 0)
-        quantize_h(256, 0)
-        quantize_x(1, 512)
-        round_wf(0, 1, 1, True)
-        quantize_wf(1, 1)
-        apply_gain(1, 0, False)
+        gather_words(0)
+        permute_w4_scales()
+        gather_words(1)
+        for h in range(2):
+            for b in range(2):
+                sigmoid_gate(h, b)
+        for i in range(PACK):
+            gather_x(0, i, 0, S)
+        load_ws(0)
+        load_ws(1)
+        load_skip(0)
+        load_skip(1)
+        apply_gain(0, 0, None)
+        gx0 = in_slot("tab", [P, PACK * S], BF16, "gx0")
+        for j0 in range(0, S, HALF):
+            round_x(0, j0, HALF, gx0[:, PACK * j0 : PACK * (j0 + HALF)])
+        round_wf(0, 0, True)
+        gather_x(1, 0, 0, S)
+        quantize_wf(0, 0, in_slot("x10", [P, PASS], U32, "wf00_codes")[:])
+        gather_x(1, 1, 0, S)
+        xg0 = in_slot("x11", [P, S], U32, "xg0")
+        quantize(xg0[:], xg_scale[:, 0, :], gx0[:])
+        for j0 in range(0, S, CHUNK):
+            xg_codes[0, j0] = xg0[:, j0 : j0 + CHUNK]
+        round_wf(1, 0, False)
+        apply_gain(0, 1, "wf10")
+        gather_x(1, 2, 0, S)
+        quantize_wf(1, 0, in_slot("x12", [P, PASS], U32, "wf10_codes")[:])
+        gather_x(1, 3, 0, HALF)
+        gather_x(1, 3, HALF, HALF)
+        h_all = in_slot("wf00", [P, 2, S], U32, "h_all")
+        wf1_codes = in_slot("picked0", [P, 2, PASS], U32, "wf1_codes")
+        round_x1(0)
+        round_x1(256)
+        quantize_x1(0, "xg1_0")
+        round_wf(0, 1, True)
+        quantize_x1(256, "wf01")
+        quantize_wf(0, 1, wf1_codes[:, 0, :])
         tanh_filter(0, 0)
-        quantize_x(1, 768)
-        tanh_filter(768, 0)
-        round_ws(0, 1, False)
-        tanh_filter(512, 0)
+        tanh_filter(256, 0)
+        round_x1(512)
+        apply_gain(1, 0, "x13")
         gated_product(0, 0)
-        quantize_ws(0)
-        apply_gain(0, 1, False)
-        gated_product(768, 0)
-        quantize_h(768, 0)
-        quantize_wf(0, 1)
-        round_ws(1, 0, False)
-        tanh_filter(0, 1)
-        gated_product(512, 0)
-        round_ws(1, 1, False)
-        quantize_ws(1)
-        gated_product(0, 1)
-        quantize_h(0, 1)
+        round_wf(1, 1, True)
         quantize_h(0, 0)
-        tanh_filter(512, 1)
-        gated_product(512, 1)
+        quantize_wf(1, 1, wf1_codes[:, 1, :])
+        gated_product(256, 0)
+        round_ws(0, True)
+        quantize_h(256, 0)
+        quantize_x1(512, "x00")
+        tanh_filter(0, 1)
         tanh_filter(256, 1)
-        quantize_h(512, 1)
+        round_ws(1, False)
+        gated_product(0, 1)
+        quantize_ws(0)
+        quantize_h(0, 1)
+        tanh_filter(512, 0)
+        round_x1(768, "x01")
+        apply_gain(1, 1, "picked1")
         gated_product(256, 1)
+        quantize_ws(1)
         quantize_h(256, 1)
-        tanh_filter(768, 1)
+        gated_product(512, 0)
+        quantize_x1(768, "xg1_3")
         skip_sum(0, 0)
-        skip_sum(256, 2)
         quantize_h(512, 0)
-        gated_product(768, 1)
-        quantize_h(768, 1)
-        skip_sum(256, 0)
         skip_sum(0, 2)
-        skip_sum(512, 2)
-        skip_sum(768, 2)
-        skip_sum(768, 0)
+        tanh_filter(512, 1)
+        tanh_filter(768, 0)
+        skip_sum(256, 0)
+        skip_sum(256, 2)
+        gated_product(512, 1)
+        tanh_filter(768, 1)
+        gated_product(768, 0)
+        quantize_h(512, 1)
+        quantize_h(768, 0)
+        gated_product(768, 1)
         skip_sum(512, 0)
+        quantize_h(768, 1)
+        skip_sum(512, 2)
+        skip_sum(768, 0)
+        skip_sum(768, 2)

@@ -225,10 +225,10 @@ def tile_list_vocoder_speaker_gate_skip_kernel(
             h_scale[j0, b] = kept([P, CHUNK], U8, "h_scale%d_%d" % (j0, b))
             quantize(h_codes[j0, b], h_scale[j0, b][:], hidden[j0, b][:])
 
-        def skip_sum(j0, n0):
+        def skip_sum(j0, n0, blocks=2, banks="share"):
             h, c0 = divmod(j0, HALF)
-            share = psum.tile([P, 2, CHUNK], F32, name="share", tag="share", bufs=8 - ACC_BUFS)
-            for c in range(n0, n0 + 2):
+            share = psum.tile([P, blocks, CHUNK], F32, name="share", tag=banks, bufs=ACC_BUFS)
+            for c in range(n0, n0 + blocks):
                 n = slice(c * P, (c + 1) * P)
                 for b in range(2):
                     nc.tensor.matmul_mx(
@@ -240,9 +240,9 @@ def tile_list_vocoder_speaker_gate_skip_kernel(
                         start=(b == 0),
                         stop=(b == 1),
                     )
-            rows = skip_sb[h][:, n0 : n0 + 2, c0 : c0 + CHUNK]
+            rows = skip_sb[h][:, n0 : n0 + blocks, c0 : c0 + CHUNK]
             nc.vector.tensor_tensor(rows, share[:], rows, ADD)
-            nc.sync.dma_start(out=out_rows[:, n0 : n0 + 2, j0 : j0 + CHUNK], in_=rows)
+            nc.sync.dma_start(out=out_rows[:, n0 : n0 + blocks, j0 : j0 + CHUNK], in_=rows)
 
         nc.vector.memset(tab_plane[:], 0)
         nc.vector.memset(w4_plane[:], 0)
@@ -350,5 +350,5 @@ def tile_list_vocoder_speaker_gate_skip_kernel(
         skip_sum(512, 0)
         quantize_h(768, 1)
         skip_sum(512, 2)
-        skip_sum(768, 0)
-        skip_sum(768, 2)
+        for c in range(4):
+            skip_sum(768, c, 1, "share" if c < 2 else "acc")

@@ -258,9 +258,9 @@ def tile_list_vocoder_speaker_gate_skip_kernel(
         nc.sync.dma_start(out=gain_sb[:], in_=gain.rearrange("(b p t) -> p b t", b=2, t=PACK))
         load_x(0, 2)
         load_x(0, 3)
-        load_wf(0, 0)
         load_x(1, 0)
         load_x(1, 1)
+        load_wf(0, 0)
         load_wf(1, 0)
         load_x(1, 2)
         load_x(1, 3)
@@ -286,12 +286,12 @@ def tile_list_vocoder_speaker_gate_skip_kernel(
         gx0 = in_slot("tab", [P, PACK * S], BF16, "gx0")
         for j0 in range(0, S, HALF):
             round_x(0, j0, HALF, gx0[:, PACK * j0 : PACK * (j0 + HALF)])
-        round_wf(0, 0, True)
         gather_x(1, 0, 0, S)
-        quantize_wf(0, 0, in_slot("x10", [P, PASS], U32, "wf00_codes")[:])
         gather_x(1, 1, 0, S)
-        xg0 = in_slot("x11", [P, S], U32, "xg0")
+        round_wf(0, 0, True)
+        xg0 = in_slot("wf00", [P, S], U32, "xg0")
         quantize(xg0[:], xg_scale[:, 0, :], gx0[:])
+        quantize_wf(0, 0, in_slot("x11", [P, PASS], U32, "wf00_codes")[:])
         for j0 in range(0, S, CHUNK):
             xg_codes[0, j0] = xg0[:, j0 : j0 + CHUNK]
         round_wf(1, 0, False)
@@ -300,7 +300,7 @@ def tile_list_vocoder_speaker_gate_skip_kernel(
         quantize_wf(1, 0, in_slot("x12", [P, PASS], U32, "wf10_codes")[:])
         gather_x(1, 3, 0, HALF)
         gather_x(1, 3, HALF, HALF)
-        h_all = in_slot("wf00", [P, 2, S], U32, "h_all")
+        h_all = in_slot("x10", [P, 2, S], U32, "h_all")
         wf1_codes = in_slot("picked0", [P, 2, PASS], U32, "wf1_codes")
         round_x1(0)
         round_x1(256)

@@ -1,6 +1,7 @@
 from contextlib import ExitStack
 
 import concourse.mybir as mybir
+from concourse.masks import make_identity
 
 K, C, H, N, T, S = 1024, 512, 1024, 512, 2048, 1024
 FLOPS = 2 * S * (K * H + C * H + H * N)
@@ -22,7 +23,23 @@ PACK = 4
 PASS = P * PACK
 HALF = 512
 CHUNK = 256
-ACC_BUFS = 4
+BANKS = 4
+KIB = 1024
+
+X_AT = [8 * KIB * k for k in range(8)]
+TAB_AT = 64 * KIB
+PICKED_AT = [72 * KIB, 88 * KIB]
+GATE_AT = 104 * KIB
+SIG_AT = 112 * KIB
+XG1_AT = 136 * KIB
+WF_CODES_AT = 140 * KIB
+WS_CODES_AT = 148 * KIB
+SCALAR_RING_AT = 152 * KIB
+GX0_AT = 184 * KIB
+WGT_AT = 192 * KIB
+VECTOR_RING_AT = 184 * KIB
+SCALAR_RING_SLOTS = 8
+VECTOR_RING_SLOTS = 10
 
 
 def tile_list_vocoder_speaker_gate_skip_kernel(
@@ -31,28 +48,37 @@ def tile_list_vocoder_speaker_gate_skip_kernel(
     nc = tc.nc
     with ExitStack() as ctx:
         keep = ctx.enter_context(tc.tile_pool(name="keep", bufs=1))
-        slots = ctx.enter_context(tc.tile_pool(name="slots", bufs=1))
-        stage = ctx.enter_context(tc.tile_pool(name="stage", bufs=3))
+        placed = ctx.enter_context(tc.tile_pool(name="placed", bufs=1))
         psum = ctx.enter_context(tc.psum_pool(name="psum", bufs=1))
 
         def kept(shape, dtype, name):
             return keep.tile(shape, dtype, name=name, align_bytes=64)
 
-        def in_slot(slot, shape, dtype, name):
-            return slots.tile(shape, dtype, name=name, tag=slot, align_bytes=64)
+        def at(offset, shape, dtype, name):
+            return placed.tile(shape, dtype, name=name, offset=offset, align_bytes=64)
 
-        def loaded(slot, shape, dtype, name, source):
-            tile = in_slot(slot, shape, dtype, name)
+        def in_ring(on_vector, shape, dtype, name):
+            tag, offset, slots = ("vring", VECTOR_RING_AT, VECTOR_RING_SLOTS) if on_vector else ("sring", SCALAR_RING_AT, SCALAR_RING_SLOTS)
+            return placed.tile(shape, dtype, name=name, tag=tag, bufs=slots, offset=offset, align_bytes=64)
+
+        def in_table_ring(shape, dtype, name):
+            return placed.tile(shape, dtype, name=name, tag="table", bufs=6, offset=SCALAR_RING_AT, align_bytes=64)
+
+        def loaded(offset, shape, dtype, name, source):
+            tile = at(offset, shape, dtype, name)
             nc.sync.dma_start(out=tile[:], in_=source)
             return tile
+
+        def bank(tag, shape):
+            return psum.tile(shape, F32, name=tag, tag=tag, bufs=BANKS)
 
         offs_sb = kept([P, S // 16], U16, "offs_sb")
         offs2_sb = kept([P, S // 16], U16, "offs2_sb")
         tab_plane = kept([P, T // 4], I32, "tab_plane")
-        w4_plane = in_slot("w4_plane", [P, H // 4], I32, "w4_plane")
-        w4_raw = kept([P, H // 2], I32, "w4_raw")
-        wgt_sb = kept([P, S], F32, "wgt_sb")
+        w4_plane = kept([P, H // 4], I32, "w4_plane")
+        w4_sb = kept([P, H // 2], I32, "w4_sb")
         gain_sb = kept([P, 2, PACK], F32, "gain_sb")
+        identity = kept([P, P], F32, "identity")
 
         x_planes = xT.rearrange("(a p i) t -> a i p t", a=2, i=PACK)
         wf_rows = wf.rearrange("(a p i) r -> a p i r", a=2, i=PACK)
@@ -61,35 +87,31 @@ def tile_list_vocoder_speaker_gate_skip_kernel(
         out_rows = out.rearrange("(c p) j -> p c j", p=P)
 
         x_sb, wf_raw, ws_raw, skip_sb = {}, {}, {}, {}
+        v_codes, v_scale, sig, gate, picked, grouped, filt, hidden = {}, {}, {}, {}, {}, {}, {}, {}
+        codes, scale = {}, {}
 
         def load_x(a, i):
-            x_sb[a, i] = loaded("x%d%d" % (a, i), [P, T], F32, "x%d%d" % (a, i), x_planes[a, i])
+            x_sb[a, i] = loaded(X_AT[PACK * a + i], [P, T], F32, "x%d%d" % (a, i), x_planes[a, i])
 
-        def load_wf(a, b):
-            wf_raw[a, b] = loaded("wf%d%d" % (a, b), [P, PACK, PASS], F32, "wf%d%d" % (a, b), wf_rows[a, :, :, b * PASS : (b + 1) * PASS])
+        def load_wf(a, b, offset):
+            wf_raw[a, b] = loaded(offset, [P, PACK, PASS], F32, "wf%d%d" % (a, b), wf_rows[a, :, :, b * PASS : (b + 1) * PASS])
 
         def load_ws(b):
-            ws_raw[b] = loaded("x0%d" % b, [P, PACK, N], F32, "ws%d" % b, ws_rows[b])
+            ws_raw[b] = loaded(X_AT[3 + b], [P, PACK, N], F32, "ws%d" % b, ws_rows[b])
 
         def load_skip(h):
-            skip_sb[h] = loaded("x0%d" % (2 + h), [P, 4, HALF], F32, "skip%d" % h, skip_rows[:, :, h * HALF : (h + 1) * HALF])
+            skip_sb[h] = loaded(X_AT[5 + 2 * h], [P, 4, HALF], F32, "skip%d" % h, skip_rows[:, :, h * HALF : (h + 1) * HALF])
 
         def load_scales(plane, scales):
             for q in range(4):
                 nc.sync.dma_start(out=plane[32 * q : 32 * q + 4, :], in_=scales[0, 4 * q : 4 * q + 4, :].bitcast(I32))
 
-        w4_codes = kept([P, 2 * H], U8, "w4_codes")
-        w4_scale = kept([P, H], U8, "w4_scale")
-        v_codes = {}
-        v_scale = kept([P, S], U8, "v_scale")
-        xg_scale = kept([P, 2, S], U8, "xg_scale")
-        wf_scale = kept([P, 2, H], U8, "wf_scale")
-        ws_codes = kept([P, 2, N], U32, "ws_codes")
-        ws_scale = kept([P, 2, N], U8, "ws_scale")
-        sig, gate, picked, grouped, filt, hidden, h_codes, h_scale, xg_codes, wf_codes = {}, {}, {}, {}, {}, {}, {}, {}, {}, {}
-
-        def quantize(codes, scale, values):
-            nc.vector.quantize_mx(out=codes.bitcast(FP8X4), scales=scale, in_=values)
+        def quantize(key, offset):
+            width = grouped[key].shape[1] // PACK
+            name = "_".join(str(part) for part in key)
+            codes[key] = at(offset, [P, width], U32, "codes_" + name)
+            scale[key] = kept([P, width], U8, "scale_" + name)
+            nc.vector.quantize_mx(out=codes[key][:].bitcast(FP8X4), scales=scale[key][:], in_=grouped[key][:])
 
         def by_runs_planes(ap):
             return ap.rearrange("p t (c i) -> p c t i", i=2)
@@ -97,54 +119,51 @@ def tile_list_vocoder_speaker_gate_skip_kernel(
         def by_runs_grouped(ap):
             return ap.rearrange("p (c i t) -> p c t i", i=2, t=PACK)
 
-        def permute_w4_words():
-            nc.vector.tensor_copy(
-                out=w4_codes[:].bitcast(U16).rearrange("p (b t m) -> p b m t", b=2, t=PACK),
-                in_=w4_raw[:].bitcast(U16).rearrange("p (b m t) -> p b m t", b=2, t=PACK),
-            )
-
-        def permute_w4_scales():
-            nc.vector.tensor_copy(
-                out=w4_scale[:].rearrange("p (b t m) -> p b m t", b=2, t=PACK),
-                in_=w4_plane[:].bitcast(U8).rearrange("p (b m t) -> p b m t", b=2, t=PACK),
-            )
-
         def list_cols(j0, width):
             return slice(j0 // 16, (j0 + width) // 16)
 
-        def gather_scales(h):
-            cols = slice(h * HALF, (h + 1) * HALF)
-            nc.vector.tensor_copy(v_scale[:, cols], tab_plane[:].bitcast(U8).indirect(offs_sb[:, list_cols(h * HALF, HALF)]))
+        def gather_scales(j0, width):
+            v_scale[j0] = in_table_ring([P, width], U8, "v_scale%d" % j0)
+            nc.vector.tensor_copy(v_scale[j0][:], tab_plane[:].bitcast(U8).indirect(offs_sb[:, list_cols(j0, width)]))
 
-        def gather_words(h):
-            v_codes[h] = in_slot("w4_plane" if h else "v_codes0", [P, HALF], U32, "v_codes%d" % h)
-            nc.vector.tensor_copy(v_codes[h][:], tab_sb[:].bitcast(U32).indirect(offs_sb[:, list_cols(h * HALF, HALF)]))
+        def gather_words(j0, width):
+            v_codes[j0] = in_table_ring([P, width], U32, "v_codes%d" % j0)
+            nc.vector.tensor_copy(v_codes[j0][:], tab_sb[:].bitcast(U32).indirect(offs_sb[:, list_cols(j0, width)]))
 
-        def sigmoid_gate(h, b):
-            cols = slice(h * HALF, (h + 1) * HALF)
-            sig[h, b] = kept([P, PACK, HALF], F32, "sig%d%d" % (h, b))
-            for t in range(PACK):
-                r0 = b * PASS + t * P
-                acc = psum.tile([P, HALF], F32, name="acc", tag="acc", bufs=ACC_BUFS)
+        def sigmoid_gate(j0, b, slot):
+            h = j0 // HALF
+            if (h, b) not in sig:
+                sig[h, b] = at(SIG_AT + 8 * KIB * slot, [P, HALF // P, PASS], F32, "sig%d%d" % (h, b))
+            for c0 in range(0, v_codes[j0].shape[1], P):
+                streams = slice(c0, c0 + P)
+                acc = bank("acc", [P, PASS])
                 nc.tensor.matmul_mx(
                     out=acc[:],
-                    lhsT=w4_codes[:, 2 * r0 : 2 * (r0 + P)].bitcast(FP4X4),
-                    lhsT_scale=w4_scale[:, r0 : r0 + P],
-                    rhs=v_codes[h][:].bitcast(FP8X4),
-                    rhs_scale=v_scale[:, cols],
+                    lhsT=v_codes[j0][:, streams].bitcast(FP8X4),
+                    lhsT_scale=v_scale[j0][:, streams],
+                    rhs=w4_sb[:].bitcast(U8)[:, 2 * b * PASS : 2 * (b + 1) * PASS].bitcast(FP4X4),
+                    rhs_scale=w4_plane[:].bitcast(U8)[:, b * PASS : (b + 1) * PASS],
                     start=True,
                     stop=True,
                 )
-                nc.scalar.activation(out=sig[h, b][:, t, :], in_=acc[:], func=ACT.Sigmoid)
+                nc.scalar.activation(
+                    out=sig[h, b][:, (j0 % HALF + c0) // P, :].rearrange("p (t m) -> p t m", t=PACK),
+                    in_=acc[:].rearrange("p (m t) -> p t m", t=PACK),
+                    func=ACT.Sigmoid,
+                )
 
-        def apply_gain(h, b, slot):
-            gate[h, b] = in_slot(slot, [P, PACK, HALF], F32, "gate%d%d" % (h, b)) if slot else sig[h, b]
-            for t in range(PACK):
-                nc.scalar.activation(out=gate[h, b][:, t, :], in_=sig[h, b][:, t, :], func=ACT.Copy, scale=gain_sb[:, b, t : t + 1])
+        def turn_and_gain(h, b, offset, planes=range(PACK)):
+            if (h, b) not in gate:
+                gate[h, b] = at(offset, [P, PACK, HALF], F32, "gate%d%d" % (h, b))
+            for t in planes:
+                turned = bank("acc", [P, HALF])
+                for u in range(HALF // P):
+                    nc.tensor.transpose(turned[:, u * P : (u + 1) * P], sig[h, b][:, u, t * P : (t + 1) * P], identity[:])
+                nc.scalar.activation(out=gate[h, b][:, t, :], in_=turned[:], func=ACT.Copy, scale=gain_sb[:, b, t : t + 1])
 
         def gather_x(a, i, j0, width):
             if a not in picked:
-                picked[a] = in_slot("picked%d" % a, [P, PACK, S], F32, "picked%d" % a)
+                picked[a] = at(PICKED_AT[a], [P, PACK, S], F32, "picked%d" % a)
             nc.vector.tensor_tensor(
                 picked[a][:, i, j0 : j0 + width],
                 x_sb[a, i][:].indirect(offs2_sb[:, list_cols(j0, width)]),
@@ -156,199 +175,181 @@ def tile_list_vocoder_speaker_gate_skip_kernel(
             copy = nc.vector.tensor_copy if on_vector else nc.scalar.copy
             copy(out=target, in_=source)
 
-        def staged(width):
-            return stage.tile([P, PACK * width], BF16, name="grouped", tag="grouped", bufs=3, align_bytes=64)
+        def round_x0():
+            grouped["x", 0] = at(GX0_AT, [P, PACK * S], BF16, "gx0")
+            for j0 in range(0, S, HALF):
+                target = grouped["x", 0][:, PACK * j0 : PACK * (j0 + HALF)]
+                round_copy(by_runs_grouped(target), by_runs_planes(picked[0][:, :, j0 : j0 + HALF]), False)
 
-        def round_x(a, j0, width, target):
-            round_copy(by_runs_grouped(target), by_runs_planes(picked[a][:, :, j0 : j0 + width]), False)
+        def round_x1(c):
+            grouped["x", 1, c] = in_ring(False, [P, PACK * CHUNK], BF16, "gx1_%d" % c)
+            source = picked[1][:, :, c * CHUNK : (c + 1) * CHUNK]
+            round_copy(by_runs_grouped(grouped["x", 1, c][:]), by_runs_planes(source), False)
 
-        def round_x1(j0, slot=None):
-            if slot:
-                grouped["x", j0] = in_slot(slot, [P, PACK * CHUNK], BF16, "gx1_held")
-            else:
-                grouped["x", j0] = stage.tile([P, PACK * CHUNK], BF16, name="gx1", tag="gx1", bufs=3, align_bytes=64)
-            round_x(1, j0, CHUNK, grouped["x", j0][:])
-
-        def quantize_x1(j0, slot):
-            xg_codes[1, j0] = in_slot(slot, [P, CHUNK], U32, "xg1_%d" % j0)[:]
-            quantize(xg_codes[1, j0], xg_scale[:, 1, j0 : j0 + CHUNK], grouped["x", j0][:])
+        def quantize_x1(c):
+            quantize(("x", 1, c), XG1_AT + KIB * c)
 
         def round_wf(a, b, on_vector):
-            grouped["wf", a, b] = staged(PASS)
+            grouped["wf", a, b] = in_ring(on_vector, [P, PACK * PASS], BF16, "gwf%d%d" % (a, b))
             target = grouped["wf", a, b][:].rearrange("p (t m i) -> p m i t", t=PACK, i=PACK)
             round_copy(target, wf_raw[a, b][:].rearrange("p i (m t) -> p m i t", t=PACK), on_vector)
 
-        def quantize_wf(a, b, codes):
-            wf_codes[a, b] = codes
-            quantize(codes, wf_scale[:, a, b * PASS : (b + 1) * PASS], grouped["wf", a, b][:])
-
         def round_ws(b, on_vector):
-            grouped["ws", b] = staged(N)
+            grouped["ws", b] = in_ring(on_vector, [P, PACK * N], BF16, "gws%d" % b)
             round_copy(by_runs_grouped(grouped["ws", b][:]), by_runs_planes(ws_raw[b][:]), on_vector)
 
-        def quantize_ws(b):
-            quantize(ws_codes[:, b, :], ws_scale[:, b, :], grouped["ws", b][:])
+        def quantize_wf(a, b):
+            quantize(("wf", a, b), WF_CODES_AT + 2 * KIB * (2 * a + b))
 
-        def tanh_filter(j0, b):
-            cols = slice(j0, j0 + CHUNK)
-            filt[j0, b] = stage.tile([P, PACK, CHUNK], F32, name="filt", tag="filt", bufs=3)
+        def quantize_ws(b):
+            quantize(("ws", b), WS_CODES_AT + 2 * KIB * b)
+
+        def tanh_filter(c, b):
+            cols = slice(c * CHUNK, (c + 1) * CHUNK)
+            filt[c, b] = in_ring(False, [P, PACK, CHUNK], F32, "filt%d%d" % (c, b))
+            moving = [(codes["x", 0][:, cols], scale["x", 0][:, cols]), (codes["x", 1, c][:], scale["x", 1, c][:])]
             for t0 in range(0, PACK, 2):
-                acc = psum.tile([P, 2, CHUNK], F32, name="acc", tag="acc", bufs=ACC_BUFS)
+                acc = bank("acc", [P, 2, CHUNK])
                 for t in range(t0, t0 + 2):
                     for a in range(2):
                         nc.tensor.matmul_mx(
                             out=acc[:, t - t0, :],
-                            lhsT=wf_codes[a, b][:, t * P : (t + 1) * P].bitcast(FP8X4),
-                            lhsT_scale=wf_scale[:, a, b * PASS + t * P : b * PASS + (t + 1) * P],
-                            rhs=xg_codes[a, j0].bitcast(FP8X4),
-                            rhs_scale=xg_scale[:, a, cols],
+                            lhsT=codes["wf", a, b][:, t * P : (t + 1) * P].bitcast(FP8X4),
+                            lhsT_scale=scale["wf", a, b][:, t * P : (t + 1) * P],
+                            rhs=moving[a][0].bitcast(FP8X4),
+                            rhs_scale=moving[a][1],
                             start=(a == 0),
                             stop=(a == 1),
                         )
-                nc.scalar.activation(out=filt[j0, b][:, t0 : t0 + 2, :], in_=acc[:], func=ACT.Tanh)
+                nc.scalar.activation(out=filt[c, b][:, t0 : t0 + 2, :], in_=acc[:], func=ACT.Tanh)
 
-        def gated_product(j0, b, slot=None):
-            h, c0 = divmod(j0, HALF)
-            if slot:
-                hidden[j0, b] = in_slot(slot, [P, PACK * CHUNK], BF16, "hidden_first")
-            else:
-                hidden[j0, b] = stage.tile([P, PACK * CHUNK], BF16, name="hidden", tag="hidden", bufs=3, align_bytes=64)
+        def gated_product(c, b):
+            h, c0 = divmod(c * CHUNK, HALF)
+            grouped["h", c, b] = in_ring(True, [P, PACK * CHUNK], BF16, "hidden%d%d" % (c, b))
             nc.vector.tensor_tensor(
-                by_runs_grouped(hidden[j0, b][:]),
-                by_runs_planes(filt[j0, b][:]),
+                by_runs_grouped(grouped["h", c, b][:]),
+                by_runs_planes(filt[c, b][:]),
                 by_runs_planes(gate[h, b][:, :, c0 : c0 + CHUNK]),
                 MULT,
             )
 
-        def quantize_h(j0, b):
-            h_codes[j0, b] = h_all[:, b, j0 : j0 + CHUNK]
-            h_scale[j0, b] = kept([P, CHUNK], U8, "h_scale%d_%d" % (j0, b))
-            quantize(h_codes[j0, b], h_scale[j0, b][:], hidden[j0, b][:])
+        def quantize_h(c, b):
+            quantize(("h", c, b), PICKED_AT[0] + 8 * KIB + KIB * (2 * c + b))
 
-        def skip_sum(j0, n0, blocks=2, banks="share"):
-            h, c0 = divmod(j0, HALF)
-            share = psum.tile([P, blocks, CHUNK], F32, name="share", tag=banks, bufs=ACC_BUFS)
-            for c in range(n0, n0 + blocks):
-                n = slice(c * P, (c + 1) * P)
+        def skip_sum(c, n0, blocks=2):
+            h, c0 = divmod(c * CHUNK, HALF)
+            share = bank("share", [P, blocks, CHUNK])
+            for m in range(n0, n0 + blocks):
+                n = slice(m * P, (m + 1) * P)
                 for b in range(2):
                     nc.tensor.matmul_mx(
-                        out=share[:, c - n0, :],
-                        lhsT=ws_codes[:, b, n].bitcast(FP8X4),
-                        lhsT_scale=ws_scale[:, b, n],
-                        rhs=h_codes[j0, b].bitcast(FP8X4),
-                        rhs_scale=h_scale[j0, b][:],
+                        out=share[:, m - n0, :],
+                        lhsT=codes["ws", b][:, n].bitcast(FP8X4),
+                        lhsT_scale=scale["ws", b][:, n],
+                        rhs=codes["h", c, b][:].bitcast(FP8X4),
+                        rhs_scale=scale["h", c, b][:],
                         start=(b == 0),
                         stop=(b == 1),
                     )
-            rows = skip_sb[h][:, n0 : n0 + blocks, c0 : c0 + CHUNK]
-            nc.vector.tensor_tensor(rows, share[:], rows, ADD)
-            nc.sync.dma_start(out=out_rows[:, n0 : n0 + blocks, j0 : j0 + CHUNK], in_=rows)
+            total = in_ring(True, [P, blocks, CHUNK], F32, "total%d%d" % (c, n0))
+            nc.vector.tensor_tensor(total[:], share[:], skip_sb[h][:, n0 : n0 + blocks, c0 : c0 + CHUNK], ADD)
+            nc.sync.dma_start(out=out_rows[:, n0 : n0 + blocks, c * CHUNK : (c + 1) * CHUNK], in_=total[:])
 
         nc.vector.memset(tab_plane[:], 0)
         nc.vector.memset(w4_plane[:], 0)
+        make_identity(nc, identity[:])
         nc.sync.dma_start(offs_sb[:], offs)
-        nc.sync.dma_start(offs2_sb[:], offs2)
-        nc.sync.dma_start(out=w4_raw[:], in_=w4_words[0].bitcast(I32))
+        tab_sb = loaded(TAB_AT, [P, T], I32, "tab_sb", tab_words[0].rearrange("p t i -> p (t i)").bitcast(I32))
         load_scales(tab_plane, tab_scales)
-        tab_sb = loaded("tab", [P, T], I32, "tab_sb", tab_words[0].rearrange("p t i -> p (t i)").bitcast(I32))
+        nc.sync.dma_start(out=w4_sb[:], in_=w4_words[0].bitcast(I32))
+        wgt_sb = loaded(WGT_AT, [P, S], F32, "wgt_sb", wgt)
         load_scales(w4_plane, w4_scales)
         load_x(0, 0)
-        nc.sync.dma_start(out=wgt_sb[:], in_=wgt)
+        nc.sync.dma_start(offs2_sb[:], offs2)
         load_x(0, 1)
         nc.sync.dma_start(out=gain_sb[:], in_=gain.rearrange("(b p t) -> p b t", b=2, t=PACK))
         load_x(0, 2)
         load_x(0, 3)
-        load_x(1, 0)
-        load_x(1, 1)
-        load_wf(0, 0)
-        load_wf(1, 0)
-        load_x(1, 2)
-        load_x(1, 3)
-        load_wf(0, 1)
-        load_wf(1, 1)
+        for i in range(PACK):
+            load_x(1, i)
 
-        permute_w4_words()
-        gather_scales(0)
-        gather_scales(1)
-        gather_words(0)
-        permute_w4_scales()
-        gather_words(1)
-        for h in range(2):
+        for j0, width in ((0, CHUNK), (CHUNK, CHUNK), (HALF, HALF)):
+            gather_words(j0, width)
+            gather_scales(j0, width)
+        load_wf(0, 0, TAB_AT)
+        for j0 in (0, CHUNK):
             for b in range(2):
-                sigmoid_gate(h, b)
+                sigmoid_gate(j0, b, b)
+        sigmoid_gate(HALF, 0, 2)
+        turn_and_gain(0, 0, GATE_AT)
+        sigmoid_gate(HALF, 1, 0)
         for i in range(PACK):
             gather_x(0, i, 0, S)
+        load_wf(1, 0, X_AT[0])
+        load_wf(0, 1, X_AT[1])
+        load_wf(1, 1, X_AT[2])
+        round_x0()
+        turn_and_gain(0, 1, PICKED_AT[0])
+        for i in range(PACK - 1):
+            gather_x(1, i, 0, S)
+        quantize(("x", 0), X_AT[6])
+        gather_x(1, 3, 0, HALF)
+        gather_x(1, 3, HALF, HALF)
         load_ws(0)
         load_ws(1)
         load_skip(0)
         load_skip(1)
-        apply_gain(0, 0, None)
-        gx0 = in_slot("tab", [P, PACK * S], BF16, "gx0")
-        for j0 in range(0, S, HALF):
-            round_x(0, j0, HALF, gx0[:, PACK * j0 : PACK * (j0 + HALF)])
-        gather_x(1, 0, 0, S)
-        gather_x(1, 1, 0, S)
-        round_wf(0, 0, True)
-        xg0 = in_slot("wf00", [P, S], U32, "xg0")
-        quantize(xg0[:], xg_scale[:, 0, :], gx0[:])
-        quantize_wf(0, 0, in_slot("x11", [P, PASS], U32, "wf00_codes")[:])
-        for j0 in range(0, S, CHUNK):
-            xg_codes[0, j0] = xg0[:, j0 : j0 + CHUNK]
-        round_wf(1, 0, False)
-        apply_gain(0, 1, "wf10")
-        gather_x(1, 2, 0, S)
-        quantize_wf(1, 0, in_slot("x12", [P, PASS], U32, "wf10_codes")[:])
-        gather_x(1, 3, 0, HALF)
-        gather_x(1, 3, HALF, HALF)
-        h_all = in_slot("x10", [P, 2, S], U32, "h_all")
-        wf1_codes = in_slot("picked0", [P, 2, PASS], U32, "wf1_codes")
+        round_wf(0, 0, False)
         round_x1(0)
-        round_x1(256)
-        quantize_x1(0, "xg1_0")
+        round_x1(1)
+        round_wf(1, 0, True)
+        quantize_wf(0, 0)
+        quantize_x1(0)
+        quantize_wf(1, 0)
         round_wf(0, 1, True)
-        quantize_x1(256, "wf01")
-        quantize_wf(0, 1, wf1_codes[:, 0, :])
+        quantize_x1(1)
+        quantize_wf(0, 1)
+        turn_and_gain(1, 0, TAB_AT)
         tanh_filter(0, 0)
-        tanh_filter(256, 0)
-        round_x1(512)
-        apply_gain(1, 0, "x13")
-        gated_product(0, 0)
+        tanh_filter(1, 0)
+        round_x1(2)
+        round_x1(3)
         round_wf(1, 1, True)
+        gated_product(0, 0)
+        quantize_wf(1, 1)
         quantize_h(0, 0)
-        quantize_wf(1, 1, wf1_codes[:, 1, :])
-        gated_product(256, 0)
-        round_ws(0, True)
-        quantize_h(256, 0)
-        quantize_x1(512, "x00")
+        gated_product(1, 0)
+        quantize_x1(2)
+        quantize_h(1, 0)
         tanh_filter(0, 1)
-        tanh_filter(256, 1)
+        round_ws(0, True)
         round_ws(1, False)
         gated_product(0, 1)
         quantize_ws(0)
         quantize_h(0, 1)
-        tanh_filter(512, 0)
-        round_x1(768, "x01")
-        apply_gain(1, 1, "picked1")
-        gated_product(256, 1)
+        tanh_filter(1, 1)
         quantize_ws(1)
-        quantize_h(256, 1)
-        gated_product(512, 0)
-        quantize_x1(768, "xg1_3")
+        quantize_x1(3)
+        tanh_filter(2, 0)
+        gated_product(1, 1)
         skip_sum(0, 0)
-        quantize_h(512, 0)
+        quantize_h(1, 1)
         skip_sum(0, 2)
-        tanh_filter(512, 1)
-        tanh_filter(768, 0)
-        skip_sum(256, 0)
-        skip_sum(256, 2)
-        gated_product(512, 1)
-        tanh_filter(768, 1)
-        gated_product(768, 0)
-        quantize_h(512, 1)
-        quantize_h(768, 0)
-        gated_product(768, 1)
-        skip_sum(512, 0)
-        quantize_h(768, 1)
-        skip_sum(512, 2)
-        for c in range(4):
-            skip_sum(768, c, 1, "share" if c < 2 else "acc")
+        turn_and_gain(1, 1, SIG_AT + 8 * KIB)
+        gated_product(2, 0)
+        skip_sum(1, 0)
+        quantize_h(2, 0)
+        skip_sum(1, 2)
+        tanh_filter(2, 1)
+        tanh_filter(3, 0)
+        tanh_filter(3, 1)
+        gated_product(2, 1)
+        gated_product(3, 0)
+        quantize_h(2, 1)
+        quantize_h(3, 0)
+        gated_product(3, 1)
+        skip_sum(2, 0)
+        quantize_h(3, 1)
+        skip_sum(2, 2)
+        for m in range(4):
+            skip_sum(3, m, 1)

@@ -210,16 +210,16 @@ def tile_list_vocoder_speaker_gate_skip_kernel(
             moving = [(codes["x", 0][:, cols], scale["x", 0][:, cols]), (codes["x", 1, c][:], scale["x", 1, c][:])]
             for t0 in range(0, PACK, 2):
                 acc = bank("acc", [P, 2, CHUNK])
-                for t in range(t0, t0 + 2):
-                    for a in range(2):
+                for a in range(2):
+                    for t in range(t0, t0 + 2):
                         nc.tensor.matmul_mx(
                             out=acc[:, t - t0, :],
                             lhsT=codes["wf", a, b][:, t * P : (t + 1) * P].bitcast(FP8X4),
                             lhsT_scale=scale["wf", a, b][:, t * P : (t + 1) * P],
                             rhs=moving[a][0].bitcast(FP8X4),
                             rhs_scale=moving[a][1],
-                            start=(a == 0),
-                            stop=(a == 1),
+                            start=(a == 0 and t == t0),
+                            stop=(a == 1 and t == t0 + 1),
                         )
                 nc.scalar.activation(out=filt[c, b][:, t0 : t0 + 2, :], in_=acc[:], func=ACT.Tanh)
 
@@ -239,17 +239,17 @@ def tile_list_vocoder_speaker_gate_skip_kernel(
         def skip_sum(c, n0, blocks=2):
             h, c0 = divmod(c * CHUNK, HALF)
             share = bank("share", [P, blocks, CHUNK])
-            for m in range(n0, n0 + blocks):
-                n = slice(m * P, (m + 1) * P)
-                for b in range(2):
+            for b in range(2):
+                for m in range(n0, n0 + blocks):
+                    n = slice(m * P, (m + 1) * P)
                     nc.tensor.matmul_mx(
                         out=share[:, m - n0, :],
                         lhsT=codes["ws", b][:, n].bitcast(FP8X4),
                         lhsT_scale=scale["ws", b][:, n],
                         rhs=codes["h", c, b][:].bitcast(FP8X4),
                         rhs_scale=scale["h", c, b][:],
-                        start=(b == 0),
-                        stop=(b == 1),
+                        start=(b == 0 and m == n0),
+                        stop=(b == 1 and m == n0 + blocks - 1),
                     )
             total = in_ring(True, [P, blocks, CHUNK], F32, "total%d%d" % (c, n0))
             nc.vector.tensor_tensor(total[:], share[:], skip_sb[h][:, n0 : n0 + blocks, c0 : c0 + CHUNK], ADD)

@@ -1,7 +1,6 @@
 from contextlib import ExitStack
 
 import concourse.mybir as mybir
-from concourse.masks import make_identity
 
 K, C, H, N, T, S = 1024, 512, 1024, 512, 2048, 1024
 FLOPS = 2 * S * (K * H + C * H + H * N)
@@ -29,17 +28,13 @@ KIB = 1024
 X_AT = [8 * KIB * k for k in range(8)]
 TAB_AT = 64 * KIB
 PICKED_AT = [72 * KIB, 88 * KIB]
-GATE_AT = 104 * KIB
-SIG_AT = 112 * KIB
-XG1_AT = 136 * KIB
-WF_CODES_AT = 140 * KIB
-WS_CODES_AT = 148 * KIB
-SCALAR_RING_AT = 152 * KIB
-GX0_AT = 184 * KIB
-WGT_AT = 192 * KIB
-VECTOR_RING_AT = 184 * KIB
+SCALAR_RING_AT = 120 * KIB
 SCALAR_RING_SLOTS = 8
-VECTOR_RING_SLOTS = 10
+VECTOR_RING_AT = 152 * KIB
+VECTOR_RING_SLOTS = 36
+SIG_AT = {(1, 0): 104 * KIB, (1, 1): 112 * KIB, (0, 0): 152 * KIB, (0, 1): 160 * KIB}
+GX0_AT = 212 * KIB
+WGT_AT = 220 * KIB
 
 
 def tile_list_vocoder_speaker_gate_skip_kernel(
@@ -78,7 +73,6 @@ def tile_list_vocoder_speaker_gate_skip_kernel(
         w4_plane = kept([P, H // 4], I32, "w4_plane")
         w4_sb = kept([P, H // 2], I32, "w4_sb")
         gain_sb = kept([P, 2, PACK], F32, "gain_sb")
-        identity = kept([P, P], F32, "identity")
 
         x_planes = xT.rearrange("(a p i) t -> a i p t", a=2, i=PACK)
         wf_rows = wf.rearrange("(a p i) r -> a p i r", a=2, i=PACK)
@@ -88,7 +82,7 @@ def tile_list_vocoder_speaker_gate_skip_kernel(
 
         x_sb, wf_raw, ws_raw, skip_sb = {}, {}, {}, {}
         v_codes, v_scale, sig, gate, picked, grouped, filt, hidden = {}, {}, {}, {}, {}, {}, {}, {}
-        codes, scale = {}, {}
+        codes, scale, w4 = {}, {}, {}
 
         def load_x(a, i):
             x_sb[a, i] = loaded(X_AT[PACK * a + i], [P, T], F32, "x%d%d" % (a, i), x_planes[a, i])
@@ -106,10 +100,10 @@ def tile_list_vocoder_speaker_gate_skip_kernel(
             for q in range(4):
                 nc.sync.dma_start(out=plane[32 * q : 32 * q + 4, :], in_=scales[0, 4 * q : 4 * q + 4, :].bitcast(I32))
 
-        def quantize(key, offset):
+        def quantize(key, offset=None):
             width = grouped[key].shape[1] // PACK
             name = "_".join(str(part) for part in key)
-            codes[key] = at(offset, [P, width], U32, "codes_" + name)
+            codes[key] = in_ring(True, [P, width], U32, "codes_" + name) if offset is None else at(offset, [P, width], U32, "codes_" + name)
             scale[key] = kept([P, width], U8, "scale_" + name)
             nc.vector.quantize_mx(out=codes[key][:].bitcast(FP8X4), scales=scale[key][:], in_=grouped[key][:])
 
@@ -130,36 +124,49 @@ def tile_list_vocoder_speaker_gate_skip_kernel(
             v_codes[j0] = in_table_ring([P, width], U32, "v_codes%d" % j0)
             nc.vector.tensor_copy(v_codes[j0][:], tab_sb[:].bitcast(U32).indirect(offs_sb[:, list_cols(j0, width)]))
 
-        def sigmoid_gate(j0, b, slot):
-            h = j0 // HALF
-            if (h, b) not in sig:
-                sig[h, b] = at(SIG_AT + 8 * KIB * slot, [P, HALF // P, PASS], F32, "sig%d%d" % (h, b))
-            for c0 in range(0, v_codes[j0].shape[1], P):
-                streams = slice(c0, c0 + P)
-                acc = bank("acc", [P, PASS])
+        def permute_w4_words():
+            w4["codes"] = in_table_ring([P, 2 * H], U8, "w4_codes")
+            nc.vector.tensor_copy(
+                out=w4["codes"][:].bitcast(U16).rearrange("p (b t m) -> p b m t", b=2, t=PACK),
+                in_=w4_sb[:].bitcast(U16).rearrange("p (b m t) -> p b m t", b=2, t=PACK),
+            )
+
+        def permute_w4_scales():
+            w4["scale"] = in_table_ring([P, H], U8, "w4_scale")
+            nc.vector.tensor_copy(
+                out=w4["scale"][:].rearrange("p (b t m) -> p b m t", b=2, t=PACK),
+                in_=w4_plane[:].bitcast(U8).rearrange("p (b m t) -> p b m t", b=2, t=PACK),
+            )
+
+        def sigmoid_gate(h, b):
+            sig[h, b] = at(SIG_AT[h, b], [P, PACK, HALF], F32, "sig%d%d" % (h, b))
+            for t in range(PACK):
+                r0 = b * PASS + t * P
+                acc = bank("acc", [P, HALF])
                 nc.tensor.matmul_mx(
                     out=acc[:],
-                    lhsT=v_codes[j0][:, streams].bitcast(FP8X4),
-                    lhsT_scale=v_scale[j0][:, streams],
-                    rhs=w4_sb[:].bitcast(U8)[:, 2 * b * PASS : 2 * (b + 1) * PASS].bitcast(FP4X4),
-                    rhs_scale=w4_plane[:].bitcast(U8)[:, b * PASS : (b + 1) * PASS],
+                    lhsT=w4["codes"][:, 2 * r0 : 2 * (r0 + P)].bitcast(FP4X4),
+                    lhsT_scale=w4["scale"][:, r0 : r0 + P],
+                    rhs=v_codes[h * HALF][:].bitcast(FP8X4),
+                    rhs_scale=v_scale[h * HALF][:],
                     start=True,
                     stop=True,
                 )
-                nc.scalar.activation(
-                    out=sig[h, b][:, (j0 % HALF + c0) // P, :].rearrange("p (t m) -> p t m", t=PACK),
-                    in_=acc[:].rearrange("p (m t) -> p t m", t=PACK),
-                    func=ACT.Sigmoid,
-                )
+                nc.scalar.activation(out=sig[h, b][:, t, :], in_=acc[:], func=ACT.Sigmoid)
 
-        def turn_and_gain(h, b, offset, planes=range(PACK)):
-            if (h, b) not in gate:
-                gate[h, b] = at(offset, [P, PACK, HALF], F32, "gate%d%d" % (h, b))
-            for t in planes:
-                turned = bank("acc", [P, HALF])
-                for u in range(HALF // P):
-                    nc.tensor.transpose(turned[:, u * P : (u + 1) * P], sig[h, b][:, u, t * P : (t + 1) * P], identity[:])
-                nc.scalar.activation(out=gate[h, b][:, t, :], in_=turned[:], func=ACT.Copy, scale=gain_sb[:, b, t : t + 1])
+        def apply_gain(target, source, b):
+            for t in range(PACK):
+                nc.scalar.activation(out=target[:, t, :], in_=source[:, t, :], func=ACT.Copy, scale=gain_sb[:, b, t : t + 1])
+
+        def gain_first_half(b):
+            both = at(PICKED_AT[0] + 8 * KIB * b, [P, PACK, HALF], F32, "gate0%d" % b)
+            apply_gain(both[:], sig[0, b][:], b)
+            for c in range(2):
+                gate[c, b] = both[:, :, c * CHUNK : (c + 1) * CHUNK]
+
+        def gain_chunk(c, b):
+            gate[c, b] = in_ring(False, [P, PACK, CHUNK], F32, "gate_c%d%d" % (c, b))[:]
+            apply_gain(gate[c, b], sig[1, b][:, :, (c - 2) * CHUNK : (c - 1) * CHUNK], b)
 
         def gather_x(a, i, j0, width):
             if a not in picked:
@@ -187,22 +194,22 @@ def tile_list_vocoder_speaker_gate_skip_kernel(
             round_copy(by_runs_grouped(grouped["x", 1, c][:]), by_runs_planes(source), False)
 
         def quantize_x1(c):
-            quantize(("x", 1, c), XG1_AT + KIB * c)
+            quantize(("x", 1, c))
 
-        def round_wf(a, b, on_vector):
-            grouped["wf", a, b] = in_ring(on_vector, [P, PACK * PASS], BF16, "gwf%d%d" % (a, b))
-            target = grouped["wf", a, b][:].rearrange("p (t m i) -> p m i t", t=PACK, i=PACK)
-            round_copy(target, wf_raw[a, b][:].rearrange("p i (m t) -> p m i t", t=PACK), on_vector)
+        def round_wf(a, b, u, on_vector):
+            grouped["wf", a, b, u] = in_ring(on_vector, [P, PACK * CHUNK], BF16, "gwf%d%d%d" % (a, b, u))
+            target = grouped["wf", a, b, u][:].rearrange("p (t m i) -> p m i t", t=2, i=PACK)
+            round_copy(target, wf_raw[a, b][:].rearrange("p i (m t) -> p m i t", t=PACK)[:, :, :, 2 * u : 2 * u + 2], on_vector)
 
-        def round_ws(b, on_vector):
-            grouped["ws", b] = in_ring(on_vector, [P, PACK * N], BF16, "gws%d" % b)
-            round_copy(by_runs_grouped(grouped["ws", b][:]), by_runs_planes(ws_raw[b][:]), on_vector)
+        def round_ws(b, u, on_vector):
+            grouped["ws", b, u] = in_ring(on_vector, [P, PACK * CHUNK], BF16, "gws%d%d" % (b, u))
+            round_copy(by_runs_grouped(grouped["ws", b, u][:]), by_runs_planes(ws_raw[b][:, :, u * CHUNK : (u + 1) * CHUNK]), on_vector)
 
-        def quantize_wf(a, b):
-            quantize(("wf", a, b), WF_CODES_AT + 2 * KIB * (2 * a + b))
+        def quantize_wf(a, b, u):
+            quantize(("wf", a, b, u))
 
-        def quantize_ws(b):
-            quantize(("ws", b), WS_CODES_AT + 2 * KIB * b)
+        def quantize_ws(b, u):
+            quantize(("ws", b, u))
 
         def tanh_filter(c, b):
             cols = slice(c * CHUNK, (c + 1) * CHUNK)
@@ -214,8 +221,8 @@ def tile_list_vocoder_speaker_gate_skip_kernel(
                     for t in range(t0, t0 + 2):
                         nc.tensor.matmul_mx(
                             out=acc[:, t - t0, :],
-                            lhsT=codes["wf", a, b][:, t * P : (t + 1) * P].bitcast(FP8X4),
-                            lhsT_scale=scale["wf", a, b][:, t * P : (t + 1) * P],
+                            lhsT=codes["wf", a, b, t // 2][:, t % 2 * P : (t % 2 + 1) * P].bitcast(FP8X4),
+                            lhsT_scale=scale["wf", a, b, t // 2][:, t % 2 * P : (t % 2 + 1) * P],
                             rhs=moving[a][0].bitcast(FP8X4),
                             rhs_scale=moving[a][1],
                             start=(a == 0 and t == t0),
@@ -224,28 +231,27 @@ def tile_list_vocoder_speaker_gate_skip_kernel(
                 nc.scalar.activation(out=filt[c, b][:, t0 : t0 + 2, :], in_=acc[:], func=ACT.Tanh)
 
         def gated_product(c, b):
-            h, c0 = divmod(c * CHUNK, HALF)
             grouped["h", c, b] = in_ring(True, [P, PACK * CHUNK], BF16, "hidden%d%d" % (c, b))
             nc.vector.tensor_tensor(
                 by_runs_grouped(grouped["h", c, b][:]),
                 by_runs_planes(filt[c, b][:]),
-                by_runs_planes(gate[h, b][:, :, c0 : c0 + CHUNK]),
+                by_runs_planes(gate[c, b]),
                 MULT,
             )
 
         def quantize_h(c, b):
-            quantize(("h", c, b), PICKED_AT[0] + 8 * KIB + KIB * (2 * c + b))
+            quantize(("h", c, b))
 
         def skip_sum(c, n0, blocks=2):
             h, c0 = divmod(c * CHUNK, HALF)
             share = bank("share", [P, blocks, CHUNK])
             for b in range(2):
                 for m in range(n0, n0 + blocks):
-                    n = slice(m * P, (m + 1) * P)
+                    n = slice(m % 2 * P, (m % 2 + 1) * P)
                     nc.tensor.matmul_mx(
                         out=share[:, m - n0, :],
-                        lhsT=codes["ws", b][:, n].bitcast(FP8X4),
-                        lhsT_scale=scale["ws", b][:, n],
+                        lhsT=codes["ws", b, m // 2][:, n].bitcast(FP8X4),
+                        lhsT_scale=scale["ws", b, m // 2][:, n],
                         rhs=codes["h", c, b][:].bitcast(FP8X4),
                         rhs_scale=scale["h", c, b][:],
                         start=(b == 0 and m == n0),
@@ -257,15 +263,14 @@ def tile_list_vocoder_speaker_gate_skip_kernel(
 
         nc.vector.memset(tab_plane[:], 0)
         nc.vector.memset(w4_plane[:], 0)
-        make_identity(nc, identity[:])
         nc.sync.dma_start(offs_sb[:], offs)
-        tab_sb = loaded(TAB_AT, [P, T], I32, "tab_sb", tab_words[0].rearrange("p t i -> p (t i)").bitcast(I32))
-        load_scales(tab_plane, tab_scales)
+        nc.sync.dma_start(offs2_sb[:], offs2)
         nc.sync.dma_start(out=w4_sb[:], in_=w4_words[0].bitcast(I32))
-        wgt_sb = loaded(WGT_AT, [P, S], F32, "wgt_sb", wgt)
+        load_scales(tab_plane, tab_scales)
+        tab_sb = loaded(TAB_AT, [P, T], I32, "tab_sb", tab_words[0].rearrange("p t i -> p (t i)").bitcast(I32))
         load_scales(w4_plane, w4_scales)
         load_x(0, 0)
-        nc.sync.dma_start(offs2_sb[:], offs2)
+        wgt_sb = loaded(WGT_AT, [P, S], F32, "wgt_sb", wgt)
         load_x(0, 1)
         nc.sync.dma_start(out=gain_sb[:], in_=gain.rearrange("(b p t) -> p b t", b=2, t=PACK))
         load_x(0, 2)
@@ -273,23 +278,24 @@ def tile_list_vocoder_speaker_gate_skip_kernel(
         for i in range(PACK):
             load_x(1, i)
 
-        for j0, width in ((0, CHUNK), (CHUNK, CHUNK), (HALF, HALF)):
-            gather_words(j0, width)
-            gather_scales(j0, width)
+        permute_w4_words()
+        gather_scales(0, HALF)
+        gather_scales(HALF, HALF)
+        gather_words(0, HALF)
+        permute_w4_scales()
+        gather_words(HALF, HALF)
         load_wf(0, 0, TAB_AT)
-        for j0 in (0, CHUNK):
+        for h in range(2):
             for b in range(2):
-                sigmoid_gate(j0, b, b)
-        sigmoid_gate(HALF, 0, 2)
-        turn_and_gain(0, 0, GATE_AT)
-        sigmoid_gate(HALF, 1, 0)
+                sigmoid_gate(h, b)
         for i in range(PACK):
             gather_x(0, i, 0, S)
         load_wf(1, 0, X_AT[0])
         load_wf(0, 1, X_AT[1])
         load_wf(1, 1, X_AT[2])
         round_x0()
-        turn_and_gain(0, 1, PICKED_AT[0])
+        gain_first_half(0)
+        gain_first_half(1)
         for i in range(PACK - 1):
             gather_x(1, i, 0, S)
         quantize(("x", 0), X_AT[6])
@@ -299,57 +305,73 @@ def tile_list_vocoder_speaker_gate_skip_kernel(
         load_ws(1)
         load_skip(0)
         load_skip(1)
-        round_wf(0, 0, False)
         round_x1(0)
         round_x1(1)
-        round_wf(1, 0, True)
-        quantize_wf(0, 0)
+        round_wf(0, 0, 0, True)
+        round_wf(0, 0, 1, True)
+        quantize_wf(0, 0, 0)
         quantize_x1(0)
-        quantize_wf(1, 0)
-        round_wf(0, 1, True)
+        quantize_wf(0, 0, 1)
+        round_wf(1, 0, 0, True)
+        round_wf(1, 0, 1, True)
+        quantize_wf(1, 0, 0)
         quantize_x1(1)
-        quantize_wf(0, 1)
-        turn_and_gain(1, 0, TAB_AT)
+        quantize_wf(1, 0, 1)
+        round_x1(2)
+        gain_chunk(2, 0)
+        gain_chunk(3, 0)
+        round_wf(0, 1, 0, True)
+        round_wf(0, 1, 1, True)
         tanh_filter(0, 0)
         tanh_filter(1, 0)
-        round_x1(2)
+        quantize_wf(0, 1, 0)
+        quantize_x1(2)
+        quantize_wf(0, 1, 1)
+        tanh_filter(2, 0)
         round_x1(3)
-        round_wf(1, 1, True)
+        round_wf(1, 1, 0, True)
+        round_wf(1, 1, 1, True)
+        quantize_wf(1, 1, 0)
         gated_product(0, 0)
-        quantize_wf(1, 1)
+        quantize_wf(1, 1, 1)
         quantize_h(0, 0)
         gated_product(1, 0)
-        quantize_x1(2)
+        quantize_x1(3)
         quantize_h(1, 0)
         tanh_filter(0, 1)
-        round_ws(0, True)
-        round_ws(1, False)
+        round_ws(0, 0, True)
+        round_ws(0, 1, True)
+        round_ws(1, 0, False)
+        round_ws(1, 1, False)
+        quantize_ws(0, 0)
+        gated_product(2, 0)
+        quantize_ws(0, 1)
+        quantize_h(2, 0)
         gated_product(0, 1)
-        quantize_ws(0)
-        quantize_h(0, 1)
         tanh_filter(1, 1)
-        quantize_ws(1)
-        quantize_x1(3)
-        tanh_filter(2, 0)
+        gain_chunk(2, 1)
+        quantize_ws(1, 0)
+        quantize_ws(1, 1)
+        quantize_h(0, 1)
+        tanh_filter(2, 1)
         gated_product(1, 1)
         skip_sum(0, 0)
         quantize_h(1, 1)
         skip_sum(0, 2)
-        turn_and_gain(1, 1, SIG_AT + 8 * KIB)
-        gated_product(2, 0)
-        skip_sum(1, 0)
-        quantize_h(2, 0)
-        skip_sum(1, 2)
-        tanh_filter(2, 1)
         tanh_filter(3, 0)
+        gain_chunk(3, 1)
         tanh_filter(3, 1)
         gated_product(2, 1)
-        gated_product(3, 0)
+        skip_sum(1, 0)
         quantize_h(2, 1)
+        gated_product(3, 0)
+        skip_sum(1, 2)
         quantize_h(3, 0)
         gated_product(3, 1)
         skip_sum(2, 0)
         quantize_h(3, 1)
         skip_sum(2, 2)
-        for m in range(4):
-            skip_sum(3, m, 1)
+        skip_sum(3, 0, 1)
+        skip_sum(3, 1, 1)
+        skip_sum(3, 2, 1)
+        skip_sum(3, 3, 1)

@@ -27,12 +27,12 @@ KIB = 1024
 
 X_AT = [8 * KIB * k for k in range(8)]
 TAB_AT = 64 * KIB
-PICKED_AT = [72 * KIB, 88 * KIB]
-SCALAR_RING_AT = 120 * KIB
-SCALAR_RING_SLOTS = 8
-VECTOR_RING_AT = 152 * KIB
-VECTOR_RING_SLOTS = 36
-SIG_AT = {(1, 0): 104 * KIB, (1, 1): 112 * KIB, (0, 0): 152 * KIB, (0, 1): 160 * KIB}
+PICKED_AT = [140 * KIB, 72 * KIB]
+SIG_AT = {(0, 0): 88 * KIB, (1, 0): 96 * KIB, (1, 1): 104 * KIB, (0, 1): 156 * KIB}
+SCALAR_RING_AT = 112 * KIB
+SCALAR_RING_SLOTS = 7
+VECTOR_RING_AT = 148 * KIB
+VECTOR_RING_SLOTS = 19
 GX0_AT = 212 * KIB
 WGT_AT = 220 * KIB
 
@@ -159,7 +159,7 @@ def tile_list_vocoder_speaker_gate_skip_kernel(
                 nc.scalar.activation(out=target[:, t, :], in_=source[:, t, :], func=ACT.Copy, scale=gain_sb[:, b, t : t + 1])
 
         def gain_first_half(b):
-            both = at(PICKED_AT[0] + 8 * KIB * b, [P, PACK, HALF], F32, "gate0%d" % b)
+            both = at(PICKED_AT[0], [P, PACK, HALF], F32, "gate01") if b else sig[0, 0]
             apply_gain(both[:], sig[0, b][:], b)
             for c in range(2):
                 gate[c, b] = both[:, :, c * CHUNK : (c + 1) * CHUNK]
@@ -196,20 +196,20 @@ def tile_list_vocoder_speaker_gate_skip_kernel(
         def quantize_x1(c):
             quantize(("x", 1, c))
 
-        def round_wf(a, b, u, on_vector):
-            grouped["wf", a, b, u] = in_ring(on_vector, [P, PACK * CHUNK], BF16, "gwf%d%d%d" % (a, b, u))
-            target = grouped["wf", a, b, u][:].rearrange("p (t m i) -> p m i t", t=2, i=PACK)
-            round_copy(target, wf_raw[a, b][:].rearrange("p i (m t) -> p m i t", t=PACK)[:, :, :, 2 * u : 2 * u + 2], on_vector)
+        def round_wf(a, b, on_vector):
+            grouped["wf", a, b] = in_ring(on_vector, [P, PACK * PASS], BF16, "gwf%d%d" % (a, b))
+            target = grouped["wf", a, b][:].rearrange("p (u e m i) -> p u m i e", u=2, e=2, i=PACK)
+            round_copy(target, wf_raw[a, b][:].rearrange("p i (m u e) -> p u m i e", u=2, e=2), on_vector)
 
-        def round_ws(b, u, on_vector):
-            grouped["ws", b, u] = in_ring(on_vector, [P, PACK * CHUNK], BF16, "gws%d%d" % (b, u))
-            round_copy(by_runs_grouped(grouped["ws", b, u][:]), by_runs_planes(ws_raw[b][:, :, u * CHUNK : (u + 1) * CHUNK]), on_vector)
+        def round_ws(b, on_vector):
+            grouped["ws", b] = in_ring(on_vector, [P, PACK * N], BF16, "gws%d" % b)
+            round_copy(by_runs_grouped(grouped["ws", b][:]), by_runs_planes(ws_raw[b][:]), on_vector)
 
-        def quantize_wf(a, b, u):
-            quantize(("wf", a, b, u))
+        def quantize_wf(a, b):
+            quantize(("wf", a, b))
 
-        def quantize_ws(b, u):
-            quantize(("ws", b, u))
+        def quantize_ws(b):
+            quantize(("ws", b))
 
         def tanh_filter(c, b):
             cols = slice(c * CHUNK, (c + 1) * CHUNK)
@@ -221,8 +221,8 @@ def tile_list_vocoder_speaker_gate_skip_kernel(
                     for t in range(t0, t0 + 2):
                         nc.tensor.matmul_mx(
                             out=acc[:, t - t0, :],
-                            lhsT=codes["wf", a, b, t // 2][:, t % 2 * P : (t % 2 + 1) * P].bitcast(FP8X4),
-                            lhsT_scale=scale["wf", a, b, t // 2][:, t % 2 * P : (t % 2 + 1) * P],
+                            lhsT=codes["wf", a, b][:, t * P : (t + 1) * P].bitcast(FP8X4),
+                            lhsT_scale=scale["wf", a, b][:, t * P : (t + 1) * P],
                             rhs=moving[a][0].bitcast(FP8X4),
                             rhs_scale=moving[a][1],
                             start=(a == 0 and t == t0),
@@ -247,11 +247,11 @@ def tile_list_vocoder_speaker_gate_skip_kernel(
             share = bank("share", [P, blocks, CHUNK])
             for b in range(2):
                 for m in range(n0, n0 + blocks):
-                    n = slice(m % 2 * P, (m % 2 + 1) * P)
+                    n = slice(m * P, (m + 1) * P)
                     nc.tensor.matmul_mx(
                         out=share[:, m - n0, :],
-                        lhsT=codes["ws", b, m // 2][:, n].bitcast(FP8X4),
-                        lhsT_scale=scale["ws", b, m // 2][:, n],
+                        lhsT=codes["ws", b][:, n].bitcast(FP8X4),
+                        lhsT_scale=scale["ws", b][:, n],
                         rhs=codes["h", c, b][:].bitcast(FP8X4),
                         rhs_scale=scale["h", c, b][:],
                         start=(b == 0 and m == n0),
@@ -293,8 +293,8 @@ def tile_list_vocoder_speaker_gate_skip_kernel(
         load_wf(1, 0, X_AT[0])
         load_wf(0, 1, X_AT[1])
         load_wf(1, 1, X_AT[2])
-        round_x0()
         gain_first_half(0)
+        round_x0()
         gain_first_half(1)
         for i in range(PACK - 1):
             gather_x(1, i, 0, S)
@@ -305,67 +305,55 @@ def tile_list_vocoder_speaker_gate_skip_kernel(
         load_ws(1)
         load_skip(0)
         load_skip(1)
+        round_wf(0, 0, False)
         round_x1(0)
         round_x1(1)
-        round_wf(0, 0, 0, True)
-        round_wf(0, 0, 1, True)
-        quantize_wf(0, 0, 0)
+        round_wf(1, 0, True)
+        quantize_wf(0, 0)
         quantize_x1(0)
-        quantize_wf(0, 0, 1)
-        round_wf(1, 0, 0, True)
-        round_wf(1, 0, 1, True)
-        quantize_wf(1, 0, 0)
+        quantize_wf(1, 0)
+        round_wf(0, 1, True)
         quantize_x1(1)
-        quantize_wf(1, 0, 1)
+        quantize_wf(0, 1)
         round_x1(2)
-        gain_chunk(2, 0)
-        gain_chunk(3, 0)
-        round_wf(0, 1, 0, True)
-        round_wf(0, 1, 1, True)
         tanh_filter(0, 0)
         tanh_filter(1, 0)
-        quantize_wf(0, 1, 0)
-        quantize_x1(2)
-        quantize_wf(0, 1, 1)
-        tanh_filter(2, 0)
         round_x1(3)
-        round_wf(1, 1, 0, True)
-        round_wf(1, 1, 1, True)
-        quantize_wf(1, 1, 0)
+        round_wf(1, 1, True)
+        quantize_x1(2)
         gated_product(0, 0)
-        quantize_wf(1, 1, 1)
+        quantize_wf(1, 1)
         quantize_h(0, 0)
-        gated_product(1, 0)
-        quantize_x1(3)
-        quantize_h(1, 0)
+        gain_chunk(2, 0)
         tanh_filter(0, 1)
-        round_ws(0, 0, True)
-        round_ws(0, 1, True)
-        round_ws(1, 0, False)
-        round_ws(1, 1, False)
-        quantize_ws(0, 0)
-        gated_product(2, 0)
-        quantize_ws(0, 1)
-        quantize_h(2, 0)
+        gated_product(1, 0)
+        round_ws(0, True)
+        quantize_h(1, 0)
+        round_ws(1, False)
+        quantize_x1(3)
         gated_product(0, 1)
-        tanh_filter(1, 1)
-        gain_chunk(2, 1)
-        quantize_ws(1, 0)
-        quantize_ws(1, 1)
+        quantize_ws(0)
         quantize_h(0, 1)
-        tanh_filter(2, 1)
+        tanh_filter(1, 1)
+        tanh_filter(2, 0)
+        quantize_ws(1)
         gated_product(1, 1)
         skip_sum(0, 0)
         quantize_h(1, 1)
         skip_sum(0, 2)
+        gain_chunk(2, 1)
+        tanh_filter(2, 1)
+        gated_product(2, 0)
+        skip_sum(1, 0)
+        quantize_h(2, 0)
+        skip_sum(1, 2)
+        gain_chunk(3, 0)
         tanh_filter(3, 0)
         gain_chunk(3, 1)
         tanh_filter(3, 1)
         gated_product(2, 1)
-        skip_sum(1, 0)
-        quantize_h(2, 1)
         gated_product(3, 0)
-        skip_sum(1, 2)
+        quantize_h(2, 1)
         quantize_h(3, 0)
         gated_product(3, 1)
         skip_sum(2, 0)

@@ -82,7 +82,7 @@ def tile_list_vocoder_speaker_gate_skip_kernel(
 
         x_sb, wf_raw, ws_raw, skip_sb = {}, {}, {}, {}
         v_codes, v_scale, sig, gate, picked, grouped, filt, hidden = {}, {}, {}, {}, {}, {}, {}, {}
-        codes, scale, w4 = {}, {}, {}
+        codes, scale, w4, ws_block = {}, {}, {}, {}
 
         def load_x(a, i):
             x_sb[a, i] = loaded(X_AT[PACK * a + i], [P, T], F32, "x%d%d" % (a, i), x_planes[a, i])
@@ -95,6 +95,8 @@ def tile_list_vocoder_speaker_gate_skip_kernel(
 
         def load_skip(h):
             skip_sb[h] = loaded(X_AT[5 + 2 * h], [P, 4, HALF], F32, "skip%d" % h, skip_rows[:, :, h * HALF : (h + 1) * HALF])
+
+        wgt_sb = at(WGT_AT, [P, S], F32, "wgt_sb")
 
         def load_scales(plane, scales):
             for q in range(4):
@@ -164,6 +166,12 @@ def tile_list_vocoder_speaker_gate_skip_kernel(
             for c in range(2):
                 gate[c, b] = both[:, :, c * CHUNK : (c + 1) * CHUNK]
 
+        def gain_chunk_on_gpsimd(c, b, offset):
+            gate[c, b] = at(offset, [P, PACK, CHUNK], F32, "gate_c%d%d" % (c, b))[:]
+            for t in range(PACK):
+                source = sig[1, b][:, t, (c - 2) * CHUNK : (c - 1) * CHUNK]
+                nc.gpsimd.tensor_scalar(gate[c, b][:, t, :], source, gain_sb[:, b, t : t + 1], 0.0, MULT, ADD)
+
         def gain_chunk(c, b):
             gate[c, b] = in_ring(False, [P, PACK, CHUNK], F32, "gate_c%d%d" % (c, b))[:]
             apply_gain(gate[c, b], sig[1, b][:, :, (c - 2) * CHUNK : (c - 1) * CHUNK], b)
@@ -201,15 +209,17 @@ def tile_list_vocoder_speaker_gate_skip_kernel(
             target = grouped["wf", a, b][:].rearrange("p (u e m i) -> p u m i e", u=2, e=2, i=PACK)
             round_copy(target, wf_raw[a, b][:].rearrange("p i (m u e) -> p u m i e", u=2, e=2), on_vector)
 
-        def round_ws(b, on_vector):
-            grouped["ws", b] = in_ring(on_vector, [P, PACK * N], BF16, "gws%d" % b)
-            round_copy(by_runs_grouped(grouped["ws", b][:]), by_runs_planes(ws_raw[b][:]), on_vector)
+        def round_ws(b, n0, width, on_vector):
+            grouped["ws", b, n0] = in_ring(on_vector, [P, PACK * width], BF16, "gws%d_%d" % (b, n0))
+            round_copy(by_runs_grouped(grouped["ws", b, n0][:]), by_runs_planes(ws_raw[b][:, :, n0 : n0 + width]), on_vector)
 
         def quantize_wf(a, b):
             quantize(("wf", a, b))
 
-        def quantize_ws(b):
-            quantize(("ws", b))
+        def quantize_ws(b, n0):
+            quantize(("ws", b, n0))
+            for m in range(codes["ws", b, n0].shape[1] // P):
+                ws_block[b, n0 // P + m] = (codes["ws", b, n0][:, m * P : (m + 1) * P], scale["ws", b, n0][:, m * P : (m + 1) * P])
 
         def tanh_filter(c, b):
             cols = slice(c * CHUNK, (c + 1) * CHUNK)
@@ -230,8 +240,9 @@ def tile_list_vocoder_speaker_gate_skip_kernel(
                         )
                 nc.scalar.activation(out=filt[c, b][:, t0 : t0 + 2, :], in_=acc[:], func=ACT.Tanh)
 
-        def gated_product(c, b):
-            grouped["h", c, b] = in_ring(True, [P, PACK * CHUNK], BF16, "hidden%d%d" % (c, b))
+        def gated_product(c, b, offset=None):
+            shape, name = [P, PACK * CHUNK], "hidden%d%d" % (c, b)
+            grouped["h", c, b] = in_ring(True, shape, BF16, name) if offset is None else at(offset, shape, BF16, name)
             nc.vector.tensor_tensor(
                 by_runs_grouped(grouped["h", c, b][:]),
                 by_runs_planes(filt[c, b][:]),
@@ -247,11 +258,10 @@ def tile_list_vocoder_speaker_gate_skip_kernel(
             share = bank("share", [P, blocks, CHUNK])
             for b in range(2):
                 for m in range(n0, n0 + blocks):
-                    n = slice(m * P, (m + 1) * P)
                     nc.tensor.matmul_mx(
                         out=share[:, m - n0, :],
-                        lhsT=codes["ws", b][:, n].bitcast(FP8X4),
-                        lhsT_scale=scale["ws", b][:, n],
+                        lhsT=ws_block[b, m][0].bitcast(FP8X4),
+                        lhsT_scale=ws_block[b, m][1],
                         rhs=codes["h", c, b][:].bitcast(FP8X4),
                         rhs_scale=scale["h", c, b][:],
                         start=(b == 0 and m == n0),
@@ -270,7 +280,7 @@ def tile_list_vocoder_speaker_gate_skip_kernel(
         tab_sb = loaded(TAB_AT, [P, T], I32, "tab_sb", tab_words[0].rearrange("p t i -> p (t i)").bitcast(I32))
         load_scales(w4_plane, w4_scales)
         load_x(0, 0)
-        wgt_sb = loaded(WGT_AT, [P, S], F32, "wgt_sb", wgt)
+        nc.sync.dma_start(out=wgt_sb[:], in_=wgt)
         load_x(0, 1)
         nc.sync.dma_start(out=gain_sb[:], in_=gain.rearrange("(b p t) -> p b t", b=2, t=PACK))
         load_x(0, 2)
@@ -316,48 +326,50 @@ def tile_list_vocoder_speaker_gate_skip_kernel(
         quantize_x1(1)
         quantize_wf(0, 1)
         round_x1(2)
+        gain_chunk(2, 0)
         tanh_filter(0, 0)
         tanh_filter(1, 0)
         round_x1(3)
         round_wf(1, 1, True)
         quantize_x1(2)
-        gated_product(0, 0)
         quantize_wf(1, 1)
-        quantize_h(0, 0)
-        gain_chunk(2, 0)
+        gated_product(0, 0)
         tanh_filter(0, 1)
+        round_ws(0, 0, CHUNK, True)
+        quantize_h(0, 0)
         gated_product(1, 0)
-        round_ws(0, True)
+        quantize_ws(0, 0)
         quantize_h(1, 0)
-        round_ws(1, False)
-        quantize_x1(3)
+        round_ws(1, 0, N, False)
         gated_product(0, 1)
-        quantize_ws(0)
-        quantize_h(0, 1)
         tanh_filter(1, 1)
+        quantize_ws(1, 0)
+        quantize_h(0, 1)
+        round_ws(0, CHUNK, CHUNK, False)
         tanh_filter(2, 0)
-        quantize_ws(1)
-        gated_product(1, 1)
-        skip_sum(0, 0)
+        gated_product(1, 1, X_AT[0])
+        quantize_ws(0, CHUNK)
         quantize_h(1, 1)
+        quantize_x1(3)
+        gain_chunk_on_gpsimd(3, 1, X_AT[0])
+        skip_sum(0, 0)
         skip_sum(0, 2)
+        skip_sum(1, 0)
+        skip_sum(1, 2)
         gain_chunk(2, 1)
         tanh_filter(2, 1)
-        gated_product(2, 0)
-        skip_sum(1, 0)
-        quantize_h(2, 0)
-        skip_sum(1, 2)
         gain_chunk(3, 0)
         tanh_filter(3, 0)
-        gain_chunk(3, 1)
         tanh_filter(3, 1)
+        gated_product(2, 0)
         gated_product(2, 1)
-        gated_product(3, 0)
+        quantize_h(2, 0)
         quantize_h(2, 1)
-        quantize_h(3, 0)
+        gated_product(3, 0)
         gated_product(3, 1)
-        skip_sum(2, 0)
+        quantize_h(3, 0)
         quantize_h(3, 1)
+        skip_sum(2, 0)
         skip_sum(2, 2)
         skip_sum(3, 0, 1)
         skip_sum(3, 1, 1)

@@ -31,8 +31,8 @@ PICKED_AT = [140 * KIB, 72 * KIB]
 SIG_AT = {(0, 0): 88 * KIB, (1, 0): 96 * KIB, (1, 1): 104 * KIB, (0, 1): 156 * KIB}
 SCALAR_RING_AT = 112 * KIB
 SCALAR_RING_SLOTS = 7
-VECTOR_RING_AT = 148 * KIB
-VECTOR_RING_SLOTS = 19
+VECTOR_RING_AT = 152 * KIB
+VECTOR_RING_SLOTS = 18
 GX0_AT = 212 * KIB
 WGT_AT = 220 * KIB
 
@@ -57,7 +57,7 @@ def tile_list_vocoder_speaker_gate_skip_kernel(
             return placed.tile(shape, dtype, name=name, tag=tag, bufs=slots, offset=offset, align_bytes=64)
 
         def in_table_ring(shape, dtype, name):
-            return placed.tile(shape, dtype, name=name, tag="table", bufs=6, offset=SCALAR_RING_AT, align_bytes=64)
+            return placed.tile(shape, dtype, name=name, tag="table", bufs=5, offset=SCALAR_RING_AT, align_bytes=64)
 
         def loaded(offset, shape, dtype, name, source):
             tile = at(offset, shape, dtype, name)
@@ -134,10 +134,10 @@ def tile_list_vocoder_speaker_gate_skip_kernel(
             )
 
         def permute_w4_scales():
-            w4["scale"] = in_table_ring([P, H], U8, "w4_scale")
-            nc.vector.tensor_copy(
-                out=w4["scale"][:].rearrange("p (b t m) -> p b m t", b=2, t=PACK),
-                in_=w4_plane[:].bitcast(U8).rearrange("p (b m t) -> p b m t", b=2, t=PACK),
+            w4["scale"] = at(SCALAR_RING_AT + 12 * KIB, [P, H], U8, "w4_scale")
+            nc.gpsimd.tensor_copy(
+                out=w4["scale"][:].rearrange("p (b t m) -> p b t m", b=2, t=PACK),
+                in_=w4_plane[:].bitcast(U8).rearrange("p (b m t) -> p b t m", b=2, t=PACK),
             )
 
         def sigmoid_gate(h, b):
@@ -172,8 +172,9 @@ def tile_list_vocoder_speaker_gate_skip_kernel(
                 source = sig[1, b][:, t, (c - 2) * CHUNK : (c - 1) * CHUNK]
                 nc.gpsimd.tensor_scalar(gate[c, b][:, t, :], source, gain_sb[:, b, t : t + 1], 0.0, MULT, ADD)
 
-        def gain_chunk(c, b):
-            gate[c, b] = in_ring(False, [P, PACK, CHUNK], F32, "gate_c%d%d" % (c, b))[:]
+        def gain_chunk(c, b, offset=None):
+            shape, name = [P, PACK, CHUNK], "gate_c%d%d" % (c, b)
+            gate[c, b] = (in_ring(False, shape, F32, name) if offset is None else at(offset, shape, F32, name))[:]
             apply_gain(gate[c, b], sig[1, b][:, :, (c - 2) * CHUNK : (c - 1) * CHUNK], b)
 
         def gather_x(a, i, j0, width):
@@ -209,8 +210,9 @@ def tile_list_vocoder_speaker_gate_skip_kernel(
             target = grouped["wf", a, b][:].rearrange("p (u e m i) -> p u m i e", u=2, e=2, i=PACK)
             round_copy(target, wf_raw[a, b][:].rearrange("p i (m u e) -> p u m i e", u=2, e=2), on_vector)
 
-        def round_ws(b, n0, width, on_vector):
-            grouped["ws", b, n0] = in_ring(on_vector, [P, PACK * width], BF16, "gws%d_%d" % (b, n0))
+        def round_ws(b, n0, width, on_vector, offset=None):
+            shape, name = [P, PACK * width], "gws%d_%d" % (b, n0)
+            grouped["ws", b, n0] = in_ring(on_vector, shape, BF16, name) if offset is None else at(offset, shape, BF16, name)
             round_copy(by_runs_grouped(grouped["ws", b, n0][:]), by_runs_planes(ws_raw[b][:, :, n0 : n0 + width]), on_vector)
 
         def quantize_wf(a, b):
@@ -253,9 +255,9 @@ def tile_list_vocoder_speaker_gate_skip_kernel(
         def quantize_h(c, b):
             quantize(("h", c, b))
 
-        def skip_sum(c, n0, blocks=2):
+        def skip_sum(c, n0, blocks=2, banks="share"):
             h, c0 = divmod(c * CHUNK, HALF)
-            share = bank("share", [P, blocks, CHUNK])
+            share = bank(banks, [P, blocks, CHUNK])
             for b in range(2):
                 for m in range(n0, n0 + blocks):
                     nc.tensor.matmul_mx(
@@ -306,6 +308,7 @@ def tile_list_vocoder_speaker_gate_skip_kernel(
         gain_first_half(0)
         round_x0()
         gain_first_half(1)
+        gain_chunk(2, 0, PICKED_AT[0] + 8 * KIB)
         for i in range(PACK - 1):
             gather_x(1, i, 0, S)
         quantize(("x", 0), X_AT[6])
@@ -326,44 +329,43 @@ def tile_list_vocoder_speaker_gate_skip_kernel(
         quantize_x1(1)
         quantize_wf(0, 1)
         round_x1(2)
-        gain_chunk(2, 0)
+        round_x1(3)
         tanh_filter(0, 0)
         tanh_filter(1, 0)
-        round_x1(3)
+        round_ws(0, 0, CHUNK, False)
         round_wf(1, 1, True)
         quantize_x1(2)
         quantize_wf(1, 1)
         gated_product(0, 0)
         tanh_filter(0, 1)
-        round_ws(0, 0, CHUNK, True)
-        quantize_h(0, 0)
+        tanh_filter(1, 1)
         gated_product(1, 0)
+        quantize_h(0, 0)
         quantize_ws(0, 0)
         quantize_h(1, 0)
-        round_ws(1, 0, N, False)
-        gated_product(0, 1)
-        tanh_filter(1, 1)
-        quantize_ws(1, 0)
-        quantize_h(0, 1)
-        round_ws(0, CHUNK, CHUNK, False)
-        tanh_filter(2, 0)
-        gated_product(1, 1, X_AT[0])
-        quantize_ws(0, CHUNK)
-        quantize_h(1, 1)
         quantize_x1(3)
-        gain_chunk_on_gpsimd(3, 1, X_AT[0])
+        round_ws(1, 0, N, False)
+        tanh_filter(2, 0)
+        gated_product(0, 1)
+        gated_product(1, 1)
+        quantize_h(0, 1)
+        quantize_h(1, 1)
+        quantize_ws(1, 0)
+        gated_product(2, 0)
+        round_ws(0, CHUNK, CHUNK, False, X_AT[4])
+        quantize_ws(0, CHUNK)
+        quantize_h(2, 0)
+        gain_chunk_on_gpsimd(3, 1, X_AT[4])
         skip_sum(0, 0)
-        skip_sum(0, 2)
         skip_sum(1, 0)
+        skip_sum(0, 2)
         skip_sum(1, 2)
         gain_chunk(2, 1)
         tanh_filter(2, 1)
         gain_chunk(3, 0)
         tanh_filter(3, 0)
         tanh_filter(3, 1)
-        gated_product(2, 0)
         gated_product(2, 1)
-        quantize_h(2, 0)
         quantize_h(2, 1)
         gated_product(3, 0)
         gated_product(3, 1)
@@ -373,5 +375,5 @@ def tile_list_vocoder_speaker_gate_skip_kernel(
         skip_sum(2, 2)
         skip_sum(3, 0, 1)
         skip_sum(3, 1, 1)
-        skip_sum(3, 2, 1)
-        skip_sum(3, 3, 1)
+        skip_sum(3, 2, 1, "acc")
+        skip_sum(3, 3, 1, "acc")

@@ -332,15 +332,16 @@ def tile_list_vocoder_speaker_gate_skip_kernel(
         round_x1(3)
         tanh_filter(0, 0)
         tanh_filter(1, 0)
-        round_ws(0, 0, CHUNK, False)
+        gain_chunk(3, 0)
         round_wf(1, 1, True)
         quantize_x1(2)
         quantize_wf(1, 1)
         gated_product(0, 0)
         tanh_filter(0, 1)
         tanh_filter(1, 1)
-        gated_product(1, 0)
+        round_ws(0, 0, CHUNK, True)
         quantize_h(0, 0)
+        gated_product(1, 0)
         quantize_ws(0, 0)
         quantize_h(1, 0)
         quantize_x1(3)
@@ -362,16 +363,15 @@ def tile_list_vocoder_speaker_gate_skip_kernel(
         skip_sum(1, 2)
         gain_chunk(2, 1)
         tanh_filter(2, 1)
-        gain_chunk(3, 0)
         tanh_filter(3, 0)
         tanh_filter(3, 1)
         gated_product(2, 1)
-        quantize_h(2, 1)
         gated_product(3, 0)
-        gated_product(3, 1)
+        quantize_h(2, 1)
         quantize_h(3, 0)
-        quantize_h(3, 1)
+        gated_product(3, 1)
         skip_sum(2, 0)
+        quantize_h(3, 1)
         skip_sum(2, 2)
         skip_sum(3, 0, 1)
         skip_sum(3, 1, 1)

@@ -82,7 +82,7 @@ def tile_list_vocoder_speaker_gate_skip_kernel(
 
         x_sb, wf_raw, ws_raw, skip_sb = {}, {}, {}, {}
         v_codes, v_scale, sig, gate, picked, grouped, filt, hidden = {}, {}, {}, {}, {}, {}, {}, {}
-        codes, scale, w4, ws_block = {}, {}, {}, {}
+        codes, scale, w4, ws_block, total = {}, {}, {}, {}, {}
 
         def load_x(a, i):
             x_sb[a, i] = loaded(X_AT[PACK * a + i], [P, T], F32, "x%d%d" % (a, i), x_planes[a, i])
@@ -97,6 +97,9 @@ def tile_list_vocoder_speaker_gate_skip_kernel(
             skip_sb[h] = loaded(X_AT[5 + 2 * h], [P, 4, HALF], F32, "skip%d" % h, skip_rows[:, :, h * HALF : (h + 1) * HALF])
 
         wgt_sb = at(WGT_AT, [P, S], F32, "wgt_sb")
+
+        def load_wgt(h):
+            nc.sync.dma_start(out=wgt_sb[:, h * HALF : (h + 1) * HALF], in_=wgt[:, h * HALF : (h + 1) * HALF])
 
         def load_scales(plane, scales):
             for q in range(4):
@@ -197,10 +200,10 @@ def tile_list_vocoder_speaker_gate_skip_kernel(
                 target = grouped["x", 0][:, PACK * j0 : PACK * (j0 + HALF)]
                 round_copy(by_runs_grouped(target), by_runs_planes(picked[0][:, :, j0 : j0 + HALF]), False)
 
-        def round_x1(c):
-            grouped["x", 1, c] = in_ring(False, [P, PACK * CHUNK], BF16, "gx1_%d" % c)
+        def round_x1(c, on_vector=False):
+            grouped["x", 1, c] = in_ring(on_vector, [P, PACK * CHUNK], BF16, "gx1_%d" % c)
             source = picked[1][:, :, c * CHUNK : (c + 1) * CHUNK]
-            round_copy(by_runs_grouped(grouped["x", 1, c][:]), by_runs_planes(source), False)
+            round_copy(by_runs_grouped(grouped["x", 1, c][:]), by_runs_planes(source), on_vector)
 
         def quantize_x1(c):
             quantize(("x", 1, c))
@@ -255,7 +258,8 @@ def tile_list_vocoder_speaker_gate_skip_kernel(
         def quantize_h(c, b):
             quantize(("h", c, b))
 
-        def skip_sum(c, n0, blocks=2, banks="share"):
+        def skip_sum(c, n0, blocks=2, banks="share", stored=None):
+            stored = stored or blocks
             h, c0 = divmod(c * CHUNK, HALF)
             share = bank(banks, [P, blocks, CHUNK])
             for b in range(2):
@@ -269,9 +273,13 @@ def tile_list_vocoder_speaker_gate_skip_kernel(
                         start=(b == 0 and m == n0),
                         stop=(b == 1 and m == n0 + blocks - 1),
                     )
-            total = in_ring(True, [P, blocks, CHUNK], F32, "total%d%d" % (c, n0))
-            nc.vector.tensor_tensor(total[:], share[:], skip_sb[h][:, n0 : n0 + blocks, c0 : c0 + CHUNK], ADD)
-            nc.sync.dma_start(out=out_rows[:, n0 : n0 + blocks, c * CHUNK : (c + 1) * CHUNK], in_=total[:])
+            first = n0 - n0 % stored
+            if n0 == first:
+                total[c] = in_ring(True, [P, stored, CHUNK], F32, "total%d%d" % (c, n0))
+            rows = total[c][:, n0 - first : n0 - first + blocks, :]
+            nc.vector.tensor_tensor(rows, share[:], skip_sb[h][:, n0 : n0 + blocks, c0 : c0 + CHUNK], ADD)
+            if n0 + blocks == first + stored:
+                nc.sync.dma_start(out=out_rows[:, first : first + stored, c * CHUNK : (c + 1) * CHUNK], in_=total[c][:])
 
         nc.vector.memset(tab_plane[:], 0)
         nc.vector.memset(w4_plane[:], 0)
@@ -281,8 +289,9 @@ def tile_list_vocoder_speaker_gate_skip_kernel(
         load_scales(tab_plane, tab_scales)
         tab_sb = loaded(TAB_AT, [P, T], I32, "tab_sb", tab_words[0].rearrange("p t i -> p (t i)").bitcast(I32))
         load_scales(w4_plane, w4_scales)
+        load_wgt(0)
         load_x(0, 0)
-        nc.sync.dma_start(out=wgt_sb[:], in_=wgt)
+        load_wgt(1)
         load_x(0, 1)
         nc.sync.dma_start(out=gain_sb[:], in_=gain.rearrange("(b p t) -> p b t", b=2, t=PACK))
         load_x(0, 2)
@@ -300,7 +309,9 @@ def tile_list_vocoder_speaker_gate_skip_kernel(
         for h in range(2):
             for b in range(2):
                 sigmoid_gate(h, b)
-        for i in range(PACK):
+        gather_x(0, 0, 0, HALF)
+        gather_x(0, 0, HALF, HALF)
+        for i in range(1, PACK):
             gather_x(0, i, 0, S)
         load_wf(1, 0, X_AT[0])
         load_wf(0, 1, X_AT[1])
@@ -320,7 +331,7 @@ def tile_list_vocoder_speaker_gate_skip_kernel(
         load_skip(1)
         round_wf(0, 0, False)
         round_x1(0)
-        round_x1(1)
+        round_x1(1, True)
         round_wf(1, 0, True)
         quantize_wf(0, 0)
         quantize_x1(0)
@@ -330,18 +341,18 @@ def tile_list_vocoder_speaker_gate_skip_kernel(
         quantize_wf(0, 1)
         round_x1(2)
         round_x1(3)
+        gain_chunk(3, 0)
         tanh_filter(0, 0)
         tanh_filter(1, 0)
-        gain_chunk(3, 0)
+        round_ws(0, 0, CHUNK, False)
         round_wf(1, 1, True)
         quantize_x1(2)
         quantize_wf(1, 1)
         gated_product(0, 0)
         tanh_filter(0, 1)
         tanh_filter(1, 1)
-        round_ws(0, 0, CHUNK, True)
-        quantize_h(0, 0)
         gated_product(1, 0)
+        quantize_h(0, 0)
         quantize_ws(0, 0)
         quantize_h(1, 0)
         quantize_x1(3)
@@ -357,9 +368,9 @@ def tile_list_vocoder_speaker_gate_skip_kernel(
         quantize_ws(0, CHUNK)
         quantize_h(2, 0)
         gain_chunk_on_gpsimd(3, 1, X_AT[4])
-        skip_sum(0, 0)
+        skip_sum(0, 0, stored=4)
         skip_sum(1, 0)
-        skip_sum(0, 2)
+        skip_sum(0, 2, stored=4)
         skip_sum(1, 2)
         gain_chunk(2, 1)
         tanh_filter(2, 1)

@@ -24,11 +24,14 @@ HALF = 512
 CHUNK = 256
 BANKS = 4
 KIB = 1024
+SCALAR, VECTOR, GPSIMD = "scalar", "vector", "gpsimd"
 
 X_AT = [8 * KIB * k for k in range(8)]
 TAB_AT = 64 * KIB
 PICKED_AT = [140 * KIB, 72 * KIB]
 SIG_AT = {(0, 0): 88 * KIB, (1, 0): 96 * KIB, (1, 1): 104 * KIB, (0, 1): 156 * KIB}
+WF_AT = {(0, 0): TAB_AT, (1, 0): X_AT[0], (0, 1): X_AT[1], (1, 1): X_AT[2]}
+HAND_OVER_AT = X_AT[6] + 4 * KIB
 SCALAR_RING_AT = 112 * KIB
 SCALAR_RING_SLOTS = 7
 VECTOR_RING_AT = 152 * KIB
@@ -52,9 +55,15 @@ def tile_list_vocoder_speaker_gate_skip_kernel(
         def at(offset, shape, dtype, name):
             return placed.tile(shape, dtype, name=name, offset=offset, align_bytes=64)
 
-        def in_ring(on_vector, shape, dtype, name):
-            tag, offset, slots = ("vring", VECTOR_RING_AT, VECTOR_RING_SLOTS) if on_vector else ("sring", SCALAR_RING_AT, SCALAR_RING_SLOTS)
-            return placed.tile(shape, dtype, name=name, tag=tag, bufs=slots, offset=offset, align_bytes=64)
+        def in_ring(engine, shape, dtype, name):
+            if engine == VECTOR:
+                return placed.tile(shape, dtype, name=name, tag="vring", bufs=VECTOR_RING_SLOTS, offset=VECTOR_RING_AT, align_bytes=64)
+            return placed.tile(shape, dtype, name=name, tag="sring", bufs=SCALAR_RING_SLOTS, offset=SCALAR_RING_AT, align_bytes=64)
+
+        def output(engine, shape, dtype, name, offset=None):
+            if engine == GPSIMD and offset is None:
+                offset = HAND_OVER_AT
+            return in_ring(engine, shape, dtype, name) if offset is None else at(offset, shape, dtype, name)
 
         def in_table_ring(shape, dtype, name):
             return placed.tile(shape, dtype, name=name, tag="table", bufs=5, offset=SCALAR_RING_AT, align_bytes=64)
@@ -73,6 +82,7 @@ def tile_list_vocoder_speaker_gate_skip_kernel(
         w4_plane = kept([P, H // 4], I32, "w4_plane")
         w4_sb = kept([P, H // 2], I32, "w4_sb")
         gain_sb = kept([P, 2, PACK], F32, "gain_sb")
+        wgt_sb = at(WGT_AT, [P, S], F32, "wgt_sb")
 
         x_planes = xT.rearrange("(a p i) t -> a i p t", a=2, i=PACK)
         wf_rows = wf.rearrange("(a p i) r -> a p i r", a=2, i=PACK)
@@ -80,15 +90,35 @@ def tile_list_vocoder_speaker_gate_skip_kernel(
         skip_rows = skip.rearrange("(c p) j -> p c j", p=P)
         out_rows = out.rearrange("(c p) j -> p c j", p=P)
 
-        x_sb, wf_raw, ws_raw, skip_sb = {}, {}, {}, {}
-        v_codes, v_scale, sig, gate, picked, grouped, filt, hidden = {}, {}, {}, {}, {}, {}, {}, {}
-        codes, scale, w4, ws_block, total = {}, {}, {}, {}, {}
+        x_sb, wf_raw, ws_raw, skip_sb, table = {}, {}, {}, {}, {}
+        v_codes, v_scale, sig, gate, picked, grouped, filt = {}, {}, {}, {}, {}, {}, {}
+        codes, scale, w4, wf_block, ws_block, total = {}, {}, {}, {}, {}, {}
+
+        def load_scales(plane, scales):
+            for q in range(4):
+                nc.sync.dma_start(out=plane[32 * q : 32 * q + 4, :], in_=scales[0, 4 * q : 4 * q + 4, :].bitcast(I32))
+
+        def load_head():
+            nc.vector.memset(tab_plane[:], 0)
+            nc.vector.memset(w4_plane[:], 0)
+            nc.sync.dma_start(offs_sb[:], offs)
+            nc.sync.dma_start(offs2_sb[:], offs2)
+            nc.sync.dma_start(out=w4_sb[:], in_=w4_words[0].bitcast(I32))
+            load_scales(tab_plane, tab_scales)
+            table["words"] = loaded(TAB_AT, [P, T], I32, "tab_sb", tab_words[0].rearrange("p t i -> p (t i)").bitcast(I32))
+            load_scales(w4_plane, w4_scales)
+
+        def load_wgt(h):
+            nc.sync.dma_start(out=wgt_sb[:, h * HALF : (h + 1) * HALF], in_=wgt[:, h * HALF : (h + 1) * HALF])
+
+        def load_gain():
+            nc.sync.dma_start(out=gain_sb[:], in_=gain.rearrange("(b p t) -> p b t", b=2, t=PACK))
 
         def load_x(a, i):
             x_sb[a, i] = loaded(X_AT[PACK * a + i], [P, T], F32, "x%d%d" % (a, i), x_planes[a, i])
 
-        def load_wf(a, b, offset):
-            wf_raw[a, b] = loaded(offset, [P, PACK, PASS], F32, "wf%d%d" % (a, b), wf_rows[a, :, :, b * PASS : (b + 1) * PASS])
+        def load_wf(a, b):
+            wf_raw[a, b] = loaded(WF_AT[a, b], [P, PACK, PASS], F32, "wf%d%d" % (a, b), wf_rows[a, :, :, b * PASS : (b + 1) * PASS])
 
         def load_ws(b):
             ws_raw[b] = loaded(X_AT[3 + b], [P, PACK, N], F32, "ws%d" % b, ws_rows[b])
@@ -96,19 +126,10 @@ def tile_list_vocoder_speaker_gate_skip_kernel(
         def load_skip(h):
             skip_sb[h] = loaded(X_AT[5 + 2 * h], [P, 4, HALF], F32, "skip%d" % h, skip_rows[:, :, h * HALF : (h + 1) * HALF])
 
-        wgt_sb = at(WGT_AT, [P, S], F32, "wgt_sb")
-
-        def load_wgt(h):
-            nc.sync.dma_start(out=wgt_sb[:, h * HALF : (h + 1) * HALF], in_=wgt[:, h * HALF : (h + 1) * HALF])
-
-        def load_scales(plane, scales):
-            for q in range(4):
-                nc.sync.dma_start(out=plane[32 * q : 32 * q + 4, :], in_=scales[0, 4 * q : 4 * q + 4, :].bitcast(I32))
-
         def quantize(key, offset=None):
             width = grouped[key].shape[1] // PACK
             name = "_".join(str(part) for part in key)
-            codes[key] = in_ring(True, [P, width], U32, "codes_" + name) if offset is None else at(offset, [P, width], U32, "codes_" + name)
+            codes[key] = output(VECTOR, [P, width], U32, "codes_" + name, offset)
             scale[key] = kept([P, width], U8, "scale_" + name)
             nc.vector.quantize_mx(out=codes[key][:].bitcast(FP8X4), scales=scale[key][:], in_=grouped[key][:])
 
@@ -121,13 +142,13 @@ def tile_list_vocoder_speaker_gate_skip_kernel(
         def list_cols(j0, width):
             return slice(j0 // 16, (j0 + width) // 16)
 
-        def gather_scales(j0, width):
-            v_scale[j0] = in_table_ring([P, width], U8, "v_scale%d" % j0)
-            nc.vector.tensor_copy(v_scale[j0][:], tab_plane[:].bitcast(U8).indirect(offs_sb[:, list_cols(j0, width)]))
+        def gather_scales(h):
+            v_scale[h] = in_table_ring([P, HALF], U8, "v_scale%d" % h)
+            nc.vector.tensor_copy(v_scale[h][:], tab_plane[:].bitcast(U8).indirect(offs_sb[:, list_cols(h * HALF, HALF)]))
 
-        def gather_words(j0, width):
-            v_codes[j0] = in_table_ring([P, width], U32, "v_codes%d" % j0)
-            nc.vector.tensor_copy(v_codes[j0][:], tab_sb[:].bitcast(U32).indirect(offs_sb[:, list_cols(j0, width)]))
+        def gather_words(h):
+            v_codes[h] = in_table_ring([P, HALF], U32, "v_codes%d" % h)
+            nc.vector.tensor_copy(v_codes[h][:], table["words"][:].bitcast(U32).indirect(offs_sb[:, list_cols(h * HALF, HALF)]))
 
         def permute_w4_words():
             w4["codes"] = in_table_ring([P, 2 * H], U8, "w4_codes")
@@ -152,33 +173,31 @@ def tile_list_vocoder_speaker_gate_skip_kernel(
                     out=acc[:],
                     lhsT=w4["codes"][:, 2 * r0 : 2 * (r0 + P)].bitcast(FP4X4),
                     lhsT_scale=w4["scale"][:, r0 : r0 + P],
-                    rhs=v_codes[h * HALF][:].bitcast(FP8X4),
-                    rhs_scale=v_scale[h * HALF][:],
+                    rhs=v_codes[h][:].bitcast(FP8X4),
+                    rhs_scale=v_scale[h][:],
                     start=True,
                     stop=True,
                 )
                 nc.scalar.activation(out=sig[h, b][:, t, :], in_=acc[:], func=ACT.Sigmoid)
 
-        def apply_gain(target, source, b):
-            for t in range(PACK):
-                nc.scalar.activation(out=target[:, t, :], in_=source[:, t, :], func=ACT.Copy, scale=gain_sb[:, b, t : t + 1])
+        def apply_gain(target, source, b, engine, planes=range(PACK)):
+            for t in planes:
+                if engine == SCALAR:
+                    nc.scalar.activation(out=target[:, t, :], in_=source[:, t, :], func=ACT.Copy, scale=gain_sb[:, b, t : t + 1])
+                else:
+                    nc.gpsimd.tensor_scalar(target[:, t, :], source[:, t, :], gain_sb[:, b, t : t + 1], 0.0, MULT, ADD)
 
         def gain_first_half(b):
             both = at(PICKED_AT[0], [P, PACK, HALF], F32, "gate01") if b else sig[0, 0]
-            apply_gain(both[:], sig[0, b][:], b)
+            apply_gain(both[:], sig[0, b][:], b, SCALAR)
             for c in range(2):
                 gate[c, b] = both[:, :, c * CHUNK : (c + 1) * CHUNK]
 
-        def gain_chunk_on_gpsimd(c, b, offset):
-            gate[c, b] = at(offset, [P, PACK, CHUNK], F32, "gate_c%d%d" % (c, b))[:]
-            for t in range(PACK):
-                source = sig[1, b][:, t, (c - 2) * CHUNK : (c - 1) * CHUNK]
-                nc.gpsimd.tensor_scalar(gate[c, b][:, t, :], source, gain_sb[:, b, t : t + 1], 0.0, MULT, ADD)
-
-        def gain_chunk(c, b, offset=None):
+        def gain_chunk(c, b, engine=SCALAR, offset=None, planes=range(PACK)):
             shape, name = [P, PACK, CHUNK], "gate_c%d%d" % (c, b)
-            gate[c, b] = (in_ring(False, shape, F32, name) if offset is None else at(offset, shape, F32, name))[:]
-            apply_gain(gate[c, b], sig[1, b][:, :, (c - 2) * CHUNK : (c - 1) * CHUNK], b)
+            if (c, b) not in gate:
+                gate[c, b] = output(engine, shape, F32, name, offset)[:]
+            apply_gain(gate[c, b], sig[1, b][:, :, (c - 2) * CHUNK : (c - 1) * CHUNK], b, engine, planes)
 
         def gather_x(a, i, j0, width):
             if a not in picked:
@@ -190,79 +209,93 @@ def tile_list_vocoder_speaker_gate_skip_kernel(
                 MULT,
             )
 
-        def round_copy(target, source, on_vector):
-            copy = nc.vector.tensor_copy if on_vector else nc.scalar.copy
+        def round_copy(target, source, engine):
+            copy = nc.vector.tensor_copy if engine == VECTOR else nc.scalar.copy
             copy(out=target, in_=source)
+
+        def round_planes(target, planes, engine):
+            if engine == GPSIMD:
+                nc.gpsimd.tensor_scalar(target.rearrange("p (c t) -> p c t", t=PACK), planes.rearrange("p t c -> p c t"), 1.0, 0.0, MULT, ADD)
+            else:
+                round_copy(by_runs_grouped(target), by_runs_planes(planes), engine)
 
         def round_x0():
             grouped["x", 0] = at(GX0_AT, [P, PACK * S], BF16, "gx0")
             for j0 in range(0, S, HALF):
-                target = grouped["x", 0][:, PACK * j0 : PACK * (j0 + HALF)]
-                round_copy(by_runs_grouped(target), by_runs_planes(picked[0][:, :, j0 : j0 + HALF]), False)
+                round_planes(grouped["x", 0][:, PACK * j0 : PACK * (j0 + HALF)], picked[0][:, :, j0 : j0 + HALF], SCALAR)
 
-        def round_x1(c, on_vector=False):
-            grouped["x", 1, c] = in_ring(on_vector, [P, PACK * CHUNK], BF16, "gx1_%d" % c)
-            source = picked[1][:, :, c * CHUNK : (c + 1) * CHUNK]
-            round_copy(by_runs_grouped(grouped["x", 1, c][:]), by_runs_planes(source), on_vector)
+        def quantize_x0():
+            quantize(("x", 0), X_AT[6])
+
+        def round_x1(c, engine, offset=None):
+            grouped["x", 1, c] = output(engine, [P, PACK * CHUNK], BF16, "gx1_%d" % c, offset)
+            round_planes(grouped["x", 1, c][:], picked[1][:, :, c * CHUNK : (c + 1) * CHUNK], engine)
 
         def quantize_x1(c):
             quantize(("x", 1, c))
 
-        def round_wf(a, b, on_vector):
-            grouped["wf", a, b] = in_ring(on_vector, [P, PACK * PASS], BF16, "gwf%d%d" % (a, b))
-            target = grouped["wf", a, b][:].rearrange("p (u e m i) -> p u m i e", u=2, e=2, i=PACK)
-            round_copy(target, wf_raw[a, b][:].rearrange("p i (m u e) -> p u m i e", u=2, e=2), on_vector)
+        def round_wf(a, b, engine, part=None, offset=None):
+            pairs = wf_raw[a, b][:].rearrange("p i (m u e) -> p u m i e", u=2, e=2)
+            if part is None:
+                grouped["wf", a, b] = output(engine, [P, PACK * PASS], BF16, "gwf%d%d" % (a, b), offset)
+                round_copy(grouped["wf", a, b][:].rearrange("p (u e m i) -> p u m i e", u=2, e=2, i=PACK), pairs, engine)
+            else:
+                grouped["wf", a, b, part] = output(engine, [P, PACK * PASS // 2], BF16, "gwf%d%d%d" % (a, b, part), offset)
+                round_copy(grouped["wf", a, b, part][:].rearrange("p (e m i) -> p m i e", e=2, i=PACK), pairs[:, part], engine)
 
-        def round_ws(b, n0, width, on_vector, offset=None):
-            shape, name = [P, PACK * width], "gws%d_%d" % (b, n0)
-            grouped["ws", b, n0] = in_ring(on_vector, shape, BF16, name) if offset is None else at(offset, shape, BF16, name)
-            round_copy(by_runs_grouped(grouped["ws", b, n0][:]), by_runs_planes(ws_raw[b][:, :, n0 : n0 + width]), on_vector)
+        def quantize_wf(a, b, part=None, offset=None):
+            if part is None:
+                quantize(("wf", a, b), offset)
+                return
+            if ("wf", a, b) not in codes:
+                codes["wf", a, b] = in_ring(VECTOR, [P, PASS], U32, "codes_wf%d%d" % (a, b))
+                scale["wf", a, b] = kept([P, PASS], U8, "scale_wf%d%d" % (a, b))
+            cols = slice(part * PASS // 2, (part + 1) * PASS // 2)
+            nc.vector.quantize_mx(out=codes["wf", a, b][:, cols].bitcast(FP8X4), scales=scale["wf", a, b][:, cols], in_=grouped["wf", a, b, part][:])
 
-        def quantize_wf(a, b):
-            quantize(("wf", a, b))
+        def round_ws(b, n0, width, engine, offset=None):
+            grouped["ws", b, n0] = output(engine, [P, PACK * width], BF16, "gws%d_%d" % (b, n0), offset)
+            round_planes(grouped["ws", b, n0][:], ws_raw[b][:, :, n0 : n0 + width], engine)
 
         def quantize_ws(b, n0):
             quantize(("ws", b, n0))
             for m in range(codes["ws", b, n0].shape[1] // P):
                 ws_block[b, n0 // P + m] = (codes["ws", b, n0][:, m * P : (m + 1) * P], scale["ws", b, n0][:, m * P : (m + 1) * P])
 
-        def tanh_filter(c, b):
-            cols = slice(c * CHUNK, (c + 1) * CHUNK)
-            filt[c, b] = in_ring(False, [P, PACK, CHUNK], F32, "filt%d%d" % (c, b))
-            moving = [(codes["x", 0][:, cols], scale["x", 0][:, cols]), (codes["x", 1, c][:], scale["x", 1, c][:])]
+        def x_operand(a, j0, width):
+            key, first = (("x", 0), j0) if a == 0 else (("x", 1, j0 // CHUNK), j0 % CHUNK)
+            return codes[key][:, first : first + width].bitcast(FP8X4), scale[key][:, first : first + width]
+
+        def tanh_filter(c, b, offset=None):
+            filt[c, b] = output(SCALAR, [P, PACK, CHUNK], F32, "filt%d%d" % (c, b), offset)
             for t0 in range(0, PACK, 2):
                 acc = bank("acc", [P, 2, CHUNK])
                 for a in range(2):
+                    x_codes, x_scale = x_operand(a, c * CHUNK, CHUNK)
                     for t in range(t0, t0 + 2):
                         nc.tensor.matmul_mx(
                             out=acc[:, t - t0, :],
                             lhsT=codes["wf", a, b][:, t * P : (t + 1) * P].bitcast(FP8X4),
                             lhsT_scale=scale["wf", a, b][:, t * P : (t + 1) * P],
-                            rhs=moving[a][0].bitcast(FP8X4),
-                            rhs_scale=moving[a][1],
+                            rhs=x_codes,
+                            rhs_scale=x_scale,
                             start=(a == 0 and t == t0),
                             stop=(a == 1 and t == t0 + 1),
                         )
                 nc.scalar.activation(out=filt[c, b][:, t0 : t0 + 2, :], in_=acc[:], func=ACT.Tanh)
 
         def gated_product(c, b, offset=None):
-            shape, name = [P, PACK * CHUNK], "hidden%d%d" % (c, b)
-            grouped["h", c, b] = in_ring(True, shape, BF16, name) if offset is None else at(offset, shape, BF16, name)
-            nc.vector.tensor_tensor(
-                by_runs_grouped(grouped["h", c, b][:]),
-                by_runs_planes(filt[c, b][:]),
-                by_runs_planes(gate[c, b]),
-                MULT,
-            )
+            grouped["h", c, b] = output(VECTOR, [P, PACK * CHUNK], BF16, "hidden%d%d" % (c, b), offset)
+            nc.vector.tensor_tensor(by_runs_grouped(grouped["h", c, b][:]), by_runs_planes(filt[c, b][:]), by_runs_planes(gate[c, b]), MULT)
 
         def quantize_h(c, b):
             quantize(("h", c, b))
 
-        def skip_sum(c, n0, blocks=2, banks="share", stored=None):
+        def skip_sum(c, n0, blocks=2, banks="share", stored=None, passes=(0, 1)):
             stored = stored or blocks
             h, c0 = divmod(c * CHUNK, HALF)
             share = bank(banks, [P, blocks, CHUNK])
-            for b in range(2):
+            for b in passes:
                 for m in range(n0, n0 + blocks):
                     nc.tensor.matmul_mx(
                         out=share[:, m - n0, :],
@@ -270,42 +303,34 @@ def tile_list_vocoder_speaker_gate_skip_kernel(
                         lhsT_scale=ws_block[b, m][1],
                         rhs=codes["h", c, b][:].bitcast(FP8X4),
                         rhs_scale=scale["h", c, b][:],
-                        start=(b == 0 and m == n0),
-                        stop=(b == 1 and m == n0 + blocks - 1),
+                        start=(b == passes[0] and m == n0),
+                        stop=(b == passes[1] and m == n0 + blocks - 1),
                     )
             first = n0 - n0 % stored
             if n0 == first:
-                total[c] = in_ring(True, [P, stored, CHUNK], F32, "total%d%d" % (c, n0))
+                total[c] = in_ring(VECTOR, [P, stored, CHUNK], F32, "total%d%d" % (c, n0))
             rows = total[c][:, n0 - first : n0 - first + blocks, :]
             nc.vector.tensor_tensor(rows, share[:], skip_sb[h][:, n0 : n0 + blocks, c0 : c0 + CHUNK], ADD)
             if n0 + blocks == first + stored:
                 nc.sync.dma_start(out=out_rows[:, first : first + stored, c * CHUNK : (c + 1) * CHUNK], in_=total[c][:])
 
-        nc.vector.memset(tab_plane[:], 0)
-        nc.vector.memset(w4_plane[:], 0)
-        nc.sync.dma_start(offs_sb[:], offs)
-        nc.sync.dma_start(offs2_sb[:], offs2)
-        nc.sync.dma_start(out=w4_sb[:], in_=w4_words[0].bitcast(I32))
-        load_scales(tab_plane, tab_scales)
-        tab_sb = loaded(TAB_AT, [P, T], I32, "tab_sb", tab_words[0].rearrange("p t i -> p (t i)").bitcast(I32))
-        load_scales(w4_plane, w4_scales)
+        load_head()
         load_wgt(0)
         load_x(0, 0)
         load_wgt(1)
         load_x(0, 1)
-        nc.sync.dma_start(out=gain_sb[:], in_=gain.rearrange("(b p t) -> p b t", b=2, t=PACK))
+        load_gain()
         load_x(0, 2)
         load_x(0, 3)
         for i in range(PACK):
             load_x(1, i)
-
         permute_w4_words()
-        gather_scales(0, HALF)
-        gather_scales(HALF, HALF)
-        gather_words(0, HALF)
+        gather_scales(0)
+        gather_scales(1)
+        gather_words(0)
         permute_w4_scales()
-        gather_words(HALF, HALF)
-        load_wf(0, 0, TAB_AT)
+        gather_words(1)
+        load_wf(0, 0)
         for h in range(2):
             for b in range(2):
                 sigmoid_gate(h, b)
@@ -313,39 +338,39 @@ def tile_list_vocoder_speaker_gate_skip_kernel(
         gather_x(0, 0, HALF, HALF)
         for i in range(1, PACK):
             gather_x(0, i, 0, S)
-        load_wf(1, 0, X_AT[0])
-        load_wf(0, 1, X_AT[1])
-        load_wf(1, 1, X_AT[2])
+        load_wf(1, 0)
+        load_wf(0, 1)
+        load_wf(1, 1)
         gain_first_half(0)
         round_x0()
         gain_first_half(1)
-        gain_chunk(2, 0, PICKED_AT[0] + 8 * KIB)
+        gain_chunk(2, 0, offset=PICKED_AT[0] + 8 * KIB)
         for i in range(PACK - 1):
             gather_x(1, i, 0, S)
-        quantize(("x", 0), X_AT[6])
+        quantize_x0()
         gather_x(1, 3, 0, HALF)
         gather_x(1, 3, HALF, HALF)
         load_ws(0)
         load_ws(1)
         load_skip(0)
         load_skip(1)
-        round_wf(0, 0, False)
-        round_x1(0)
-        round_x1(1, True)
-        round_wf(1, 0, True)
+        round_wf(0, 0, SCALAR)
+        round_x1(0, SCALAR)
+        round_x1(1, VECTOR)
+        round_wf(1, 0, VECTOR)
         quantize_wf(0, 0)
         quantize_x1(0)
         quantize_wf(1, 0)
-        round_wf(0, 1, True)
+        round_wf(0, 1, VECTOR)
         quantize_x1(1)
         quantize_wf(0, 1)
-        round_x1(2)
-        round_x1(3)
+        round_x1(2, SCALAR)
+        round_x1(3, SCALAR)
         gain_chunk(3, 0)
         tanh_filter(0, 0)
         tanh_filter(1, 0)
-        round_ws(0, 0, CHUNK, False)
-        round_wf(1, 1, True)
+        round_ws(0, 0, CHUNK, SCALAR)
+        round_wf(1, 1, VECTOR)
         quantize_x1(2)
         quantize_wf(1, 1)
         gated_product(0, 0)
@@ -356,7 +381,7 @@ def tile_list_vocoder_speaker_gate_skip_kernel(
         quantize_ws(0, 0)
         quantize_h(1, 0)
         quantize_x1(3)
-        round_ws(1, 0, N, False)
+        round_ws(1, 0, N, SCALAR)
         tanh_filter(2, 0)
         gated_product(0, 1)
         gated_product(1, 1)
@@ -364,14 +389,14 @@ def tile_list_vocoder_speaker_gate_skip_kernel(
         quantize_h(1, 1)
         quantize_ws(1, 0)
         gated_product(2, 0)
-        round_ws(0, CHUNK, CHUNK, False, X_AT[4])
+        round_ws(0, CHUNK, CHUNK, SCALAR, X_AT[4])
         quantize_ws(0, CHUNK)
         quantize_h(2, 0)
-        gain_chunk_on_gpsimd(3, 1, X_AT[4])
+        gain_chunk(3, 1, GPSIMD, X_AT[4])
         skip_sum(0, 0, stored=4)
         skip_sum(1, 0)
-        skip_sum(0, 2, stored=4)
-        skip_sum(1, 2)
+        skip_sum(0, 2, stored=4, passes=(1, 0))
+        skip_sum(1, 2, passes=(1, 0))
         gain_chunk(2, 1)
         tanh_filter(2, 1)
         tanh_filter(3, 0)

from contextlib import ExitStack

import concourse.mybir as mybir

K, C, H, N, T, S = 1024, 512, 1024, 512, 2048, 1024
FLOPS = 2 * S * (K * H + C * H + H * N)

F32 = mybir.dt.float32
BF16 = mybir.dt.bfloat16
I32 = mybir.dt.int32
U32 = mybir.dt.uint32
U16 = mybir.dt.uint16
U8 = mybir.dt.uint8
FP8X4 = mybir.dt.float8_e4m3fn_x4
FP4X4 = mybir.dt.float4_e2m1fn_x4
MULT = mybir.AluOpType.mult
ADD = mybir.AluOpType.add
ACT = mybir.ActivationFunctionType

P = 128
PACK = 4
PASS = P * PACK
HALF = 512
CHUNK = 256
BANKS = 4
KIB = 1024
SCALAR, VECTOR, GPSIMD = "scalar", "vector", "gpsimd"

X_AT = [8 * KIB * k for k in range(8)]
TAB_AT = 64 * KIB
PICKED_AT = [140 * KIB, 72 * KIB]
SIG_AT = {(0, 0): 88 * KIB, (1, 0): 96 * KIB, (1, 1): 104 * KIB, (0, 1): 156 * KIB}
WF_AT = {(0, 0): TAB_AT, (1, 0): X_AT[0], (0, 1): X_AT[1], (1, 1): X_AT[2]}
HAND_OVER_AT = X_AT[6] + 4 * KIB
SCALAR_RING_AT = 112 * KIB
SCALAR_RING_SLOTS = 7
VECTOR_RING_AT = 152 * KIB
VECTOR_RING_SLOTS = 18
GX0_AT = 212 * KIB
WGT_AT = 220 * KIB


def tile_list_vocoder_speaker_gate_skip_kernel(
    tc, xT, wgt, offs2, tab_words, tab_scales, offs, wf, w4_words, w4_scales, gain, ws, skip, out
):
    nc = tc.nc
    with ExitStack() as ctx:
        keep = ctx.enter_context(tc.tile_pool(name="keep", bufs=1))
        placed = ctx.enter_context(tc.tile_pool(name="placed", bufs=1))
        psum = ctx.enter_context(tc.psum_pool(name="psum", bufs=1))

        def kept(shape, dtype, name):
            return keep.tile(shape, dtype, name=name, align_bytes=64)

        def at(offset, shape, dtype, name):
            return placed.tile(shape, dtype, name=name, offset=offset, align_bytes=64)

        def in_ring(engine, shape, dtype, name):
            if engine == VECTOR:
                return placed.tile(shape, dtype, name=name, tag="vring", bufs=VECTOR_RING_SLOTS, offset=VECTOR_RING_AT, align_bytes=64)
            return placed.tile(shape, dtype, name=name, tag="sring", bufs=SCALAR_RING_SLOTS, offset=SCALAR_RING_AT, align_bytes=64)

        def output(engine, shape, dtype, name, offset=None):
            if engine == GPSIMD and offset is None:
                offset = HAND_OVER_AT
            return in_ring(engine, shape, dtype, name) if offset is None else at(offset, shape, dtype, name)

        def in_table_ring(shape, dtype, name):
            return placed.tile(shape, dtype, name=name, tag="table", bufs=5, offset=SCALAR_RING_AT, align_bytes=64)

        def loaded(offset, shape, dtype, name, source):
            tile = at(offset, shape, dtype, name)
            nc.sync.dma_start(out=tile[:], in_=source)
            return tile

        def bank(tag, shape):
            return psum.tile(shape, F32, name=tag, tag=tag, bufs=BANKS)

        offs_sb = kept([P, S // 16], U16, "offs_sb")
        offs2_sb = kept([P, S // 16], U16, "offs2_sb")
        tab_plane = kept([P, T // 4], I32, "tab_plane")
        w4_plane = kept([P, H // 4], I32, "w4_plane")
        w4_sb = kept([P, H // 2], I32, "w4_sb")
        gain_sb = kept([P, 2, PACK], F32, "gain_sb")
        wgt_sb = at(WGT_AT, [P, S], F32, "wgt_sb")

        x_planes = xT.rearrange("(a p i) t -> a i p t", a=2, i=PACK)
        wf_rows = wf.rearrange("(a p i) r -> a p i r", a=2, i=PACK)
        ws_rows = ws.rearrange("(b p i) n -> b p i n", b=2, i=PACK)
        skip_rows = skip.rearrange("(c p) j -> p c j", p=P)
        out_rows = out.rearrange("(c p) j -> p c j", p=P)

        x_sb, wf_raw, ws_raw, skip_sb, table = {}, {}, {}, {}, {}
        v_codes, v_scale, sig, gate, picked, grouped, filt = {}, {}, {}, {}, {}, {}, {}
        codes, scale, w4, wf_block, ws_block, total = {}, {}, {}, {}, {}, {}

        def load_scales(plane, scales):
            for q in range(4):
                nc.sync.dma_start(out=plane[32 * q : 32 * q + 4, :], in_=scales[0, 4 * q : 4 * q + 4, :].bitcast(I32))

        def load_head():
            nc.vector.memset(tab_plane[:], 0)
            nc.vector.memset(w4_plane[:], 0)
            nc.sync.dma_start(offs_sb[:], offs)
            nc.sync.dma_start(offs2_sb[:], offs2)
            nc.sync.dma_start(out=w4_sb[:], in_=w4_words[0].bitcast(I32))
            load_scales(tab_plane, tab_scales)
            table["words"] = loaded(TAB_AT, [P, T], I32, "tab_sb", tab_words[0].rearrange("p t i -> p (t i)").bitcast(I32))
            load_scales(w4_plane, w4_scales)

        def load_wgt(h):
            nc.sync.dma_start(out=wgt_sb[:, h * HALF : (h + 1) * HALF], in_=wgt[:, h * HALF : (h + 1) * HALF])

        def load_gain():
            nc.sync.dma_start(out=gain_sb[:], in_=gain.rearrange("(b p t) -> p b t", b=2, t=PACK))

        def load_x(a, i):
            x_sb[a, i] = loaded(X_AT[PACK * a + i], [P, T], F32, "x%d%d" % (a, i), x_planes[a, i])

        def load_wf(a, b):
            wf_raw[a, b] = loaded(WF_AT[a, b], [P, PACK, PASS], F32, "wf%d%d" % (a, b), wf_rows[a, :, :, b * PASS : (b + 1) * PASS])

        def load_ws(b):
            ws_raw[b] = loaded(X_AT[3 + b], [P, PACK, N], F32, "ws%d" % b, ws_rows[b])

        def load_skip(h):
            skip_sb[h] = loaded(X_AT[5 + 2 * h], [P, 4, HALF], F32, "skip%d" % h, skip_rows[:, :, h * HALF : (h + 1) * HALF])

        def quantize(key, offset=None):
            width = grouped[key].shape[1] // PACK
            name = "_".join(str(part) for part in key)
            codes[key] = output(VECTOR, [P, width], U32, "codes_" + name, offset)
            scale[key] = kept([P, width], U8, "scale_" + name)
            nc.vector.quantize_mx(out=codes[key][:].bitcast(FP8X4), scales=scale[key][:], in_=grouped[key][:])

        def by_runs_planes(ap):
            return ap.rearrange("p t (c i) -> p c t i", i=2)

        def by_runs_grouped(ap):
            return ap.rearrange("p (c i t) -> p c t i", i=2, t=PACK)

        def list_cols(j0, width):
            return slice(j0 // 16, (j0 + width) // 16)

        def gather_scales(h):
            v_scale[h] = in_table_ring([P, HALF], U8, "v_scale%d" % h)
            nc.vector.tensor_copy(v_scale[h][:], tab_plane[:].bitcast(U8).indirect(offs_sb[:, list_cols(h * HALF, HALF)]))

        def gather_words(h):
            v_codes[h] = in_table_ring([P, HALF], U32, "v_codes%d" % h)
            nc.vector.tensor_copy(v_codes[h][:], table["words"][:].bitcast(U32).indirect(offs_sb[:, list_cols(h * HALF, HALF)]))

        def permute_w4_words():
            w4["codes"] = in_table_ring([P, 2 * H], U8, "w4_codes")
            nc.vector.tensor_copy(
                out=w4["codes"][:].bitcast(U16).rearrange("p (b t m) -> p b m t", b=2, t=PACK),
                in_=w4_sb[:].bitcast(U16).rearrange("p (b m t) -> p b m t", b=2, t=PACK),
            )

        def permute_w4_scales():
            w4["scale"] = at(SCALAR_RING_AT + 12 * KIB, [P, H], U8, "w4_scale")
            nc.gpsimd.tensor_copy(
                out=w4["scale"][:].rearrange("p (b t m) -> p b t m", b=2, t=PACK),
                in_=w4_plane[:].bitcast(U8).rearrange("p (b m t) -> p b t m", b=2, t=PACK),
            )

        def sigmoid_gate(h, b):
            sig[h, b] = at(SIG_AT[h, b], [P, PACK, HALF], F32, "sig%d%d" % (h, b))
            for t in range(PACK):
                r0 = b * PASS + t * P
                acc = bank("acc", [P, HALF])
                nc.tensor.matmul_mx(
                    out=acc[:],
                    lhsT=w4["codes"][:, 2 * r0 : 2 * (r0 + P)].bitcast(FP4X4),
                    lhsT_scale=w4["scale"][:, r0 : r0 + P],
                    rhs=v_codes[h][:].bitcast(FP8X4),
                    rhs_scale=v_scale[h][:],
                    start=True,
                    stop=True,
                )
                nc.scalar.activation(out=sig[h, b][:, t, :], in_=acc[:], func=ACT.Sigmoid)

        def apply_gain(target, source, b, engine, planes=range(PACK)):
            for t in planes:
                if engine == SCALAR:
                    nc.scalar.activation(out=target[:, t, :], in_=source[:, t, :], func=ACT.Copy, scale=gain_sb[:, b, t : t + 1])
                else:
                    nc.gpsimd.tensor_scalar(target[:, t, :], source[:, t, :], gain_sb[:, b, t : t + 1], 0.0, MULT, ADD)

        def gain_first_half(b):
            both = at(PICKED_AT[0], [P, PACK, HALF], F32, "gate01") if b else sig[0, 0]
            apply_gain(both[:], sig[0, b][:], b, SCALAR)
            for c in range(2):
                gate[c, b] = both[:, :, c * CHUNK : (c + 1) * CHUNK]

        def gain_chunk(c, b, engine=SCALAR, offset=None, planes=range(PACK)):
            shape, name = [P, PACK, CHUNK], "gate_c%d%d" % (c, b)
            if (c, b) not in gate:
                gate[c, b] = output(engine, shape, F32, name, offset)[:]
            apply_gain(gate[c, b], sig[1, b][:, :, (c - 2) * CHUNK : (c - 1) * CHUNK], b, engine, planes)

        def gather_x(a, i, j0, width):
            if a not in picked:
                picked[a] = at(PICKED_AT[a], [P, PACK, S], F32, "picked%d" % a)
            nc.vector.tensor_tensor(
                picked[a][:, i, j0 : j0 + width],
                x_sb[a, i][:].indirect(offs2_sb[:, list_cols(j0, width)]),
                wgt_sb[:, j0 : j0 + width],
                MULT,
            )

        def round_copy(target, source, engine):
            copy = nc.vector.tensor_copy if engine == VECTOR else nc.scalar.copy
            copy(out=target, in_=source)

        def round_planes(target, planes, engine):
            if engine == GPSIMD:
                nc.gpsimd.tensor_scalar(target.rearrange("p (c t) -> p c t", t=PACK), planes.rearrange("p t c -> p c t"), 1.0, 0.0, MULT, ADD)
            else:
                round_copy(by_runs_grouped(target), by_runs_planes(planes), engine)

        def round_x0():
            grouped["x", 0] = at(GX0_AT, [P, PACK * S], BF16, "gx0")
            for j0 in range(0, S, HALF):
                round_planes(grouped["x", 0][:, PACK * j0 : PACK * (j0 + HALF)], picked[0][:, :, j0 : j0 + HALF], SCALAR)

        def quantize_x0():
            quantize(("x", 0), X_AT[6])

        def round_x1(c, engine, offset=None):
            grouped["x", 1, c] = output(engine, [P, PACK * CHUNK], BF16, "gx1_%d" % c, offset)
            round_planes(grouped["x", 1, c][:], picked[1][:, :, c * CHUNK : (c + 1) * CHUNK], engine)

        def quantize_x1(c):
            quantize(("x", 1, c))

        def round_wf(a, b, engine, part=None, offset=None):
            pairs = wf_raw[a, b][:].rearrange("p i (m u e) -> p u m i e", u=2, e=2)
            if part is None:
                grouped["wf", a, b] = output(engine, [P, PACK * PASS], BF16, "gwf%d%d" % (a, b), offset)
                round_copy(grouped["wf", a, b][:].rearrange("p (u e m i) -> p u m i e", u=2, e=2, i=PACK), pairs, engine)
            else:
                grouped["wf", a, b, part] = output(engine, [P, PACK * PASS // 2], BF16, "gwf%d%d%d" % (a, b, part), offset)
                round_copy(grouped["wf", a, b, part][:].rearrange("p (e m i) -> p m i e", e=2, i=PACK), pairs[:, part], engine)

        def quantize_wf(a, b, part=None, offset=None):
            if part is None:
                quantize(("wf", a, b), offset)
                return
            if ("wf", a, b) not in codes:
                codes["wf", a, b] = in_ring(VECTOR, [P, PASS], U32, "codes_wf%d%d" % (a, b))
                scale["wf", a, b] = kept([P, PASS], U8, "scale_wf%d%d" % (a, b))
            cols = slice(part * PASS // 2, (part + 1) * PASS // 2)
            nc.vector.quantize_mx(out=codes["wf", a, b][:, cols].bitcast(FP8X4), scales=scale["wf", a, b][:, cols], in_=grouped["wf", a, b, part][:])

        def round_ws(b, n0, width, engine, offset=None):
            grouped["ws", b, n0] = output(engine, [P, PACK * width], BF16, "gws%d_%d" % (b, n0), offset)
            round_planes(grouped["ws", b, n0][:], ws_raw[b][:, :, n0 : n0 + width], engine)

        def quantize_ws(b, n0):
            quantize(("ws", b, n0))
            for m in range(codes["ws", b, n0].shape[1] // P):
                ws_block[b, n0 // P + m] = (codes["ws", b, n0][:, m * P : (m + 1) * P], scale["ws", b, n0][:, m * P : (m + 1) * P])

        def x_operand(a, j0, width):
            key, first = (("x", 0), j0) if a == 0 else (("x", 1, j0 // CHUNK), j0 % CHUNK)
            return codes[key][:, first : first + width].bitcast(FP8X4), scale[key][:, first : first + width]

        def tanh_filter(c, b, offset=None):
            filt[c, b] = output(SCALAR, [P, PACK, CHUNK], F32, "filt%d%d" % (c, b), offset)
            for t0 in range(0, PACK, 2):
                acc = bank("acc", [P, 2, CHUNK])
                for a in range(2):
                    x_codes, x_scale = x_operand(a, c * CHUNK, CHUNK)
                    for t in range(t0, t0 + 2):
                        nc.tensor.matmul_mx(
                            out=acc[:, t - t0, :],
                            lhsT=codes["wf", a, b][:, t * P : (t + 1) * P].bitcast(FP8X4),
                            lhsT_scale=scale["wf", a, b][:, t * P : (t + 1) * P],
                            rhs=x_codes,
                            rhs_scale=x_scale,
                            start=(a == 0 and t == t0),
                            stop=(a == 1 and t == t0 + 1),
                        )
                nc.scalar.activation(out=filt[c, b][:, t0 : t0 + 2, :], in_=acc[:], func=ACT.Tanh)

        def gated_product(c, b, offset=None):
            grouped["h", c, b] = output(VECTOR, [P, PACK * CHUNK], BF16, "hidden%d%d" % (c, b), offset)
            nc.vector.tensor_tensor(by_runs_grouped(grouped["h", c, b][:]), by_runs_planes(filt[c, b][:]), by_runs_planes(gate[c, b]), MULT)

        def quantize_h(c, b):
            quantize(("h", c, b))

        def skip_sum(c, n0, blocks=2, banks="share", stored=None, passes=(0, 1)):
            stored = stored or blocks
            h, c0 = divmod(c * CHUNK, HALF)
            share = bank(banks, [P, blocks, CHUNK])
            for b in passes:
                for m in range(n0, n0 + blocks):
                    nc.tensor.matmul_mx(
                        out=share[:, m - n0, :],
                        lhsT=ws_block[b, m][0].bitcast(FP8X4),
                        lhsT_scale=ws_block[b, m][1],
                        rhs=codes["h", c, b][:].bitcast(FP8X4),
                        rhs_scale=scale["h", c, b][:],
                        start=(b == passes[0] and m == n0),
                        stop=(b == passes[1] and m == n0 + blocks - 1),
                    )
            first = n0 - n0 % stored
            if n0 == first:
                total[c] = in_ring(VECTOR, [P, stored, CHUNK], F32, "total%d%d" % (c, n0))
            rows = total[c][:, n0 - first : n0 - first + blocks, :]
            nc.vector.tensor_tensor(rows, share[:], skip_sb[h][:, n0 : n0 + blocks, c0 : c0 + CHUNK], ADD)
            if n0 + blocks == first + stored:
                nc.sync.dma_start(out=out_rows[:, first : first + stored, c * CHUNK : (c + 1) * CHUNK], in_=total[c][:])

        load_head()
        load_wgt(0)
        load_x(0, 0)
        load_wgt(1)
        load_x(0, 1)
        load_gain()
        load_x(0, 2)
        load_x(0, 3)
        for i in range(PACK):
            load_x(1, i)
        permute_w4_words()
        gather_scales(0)
        gather_scales(1)
        gather_words(0)
        permute_w4_scales()
        gather_words(1)
        load_wf(0, 0)
        for h in range(2):
            for b in range(2):
                sigmoid_gate(h, b)
        gather_x(0, 0, 0, HALF)
        gather_x(0, 0, HALF, HALF)
        for i in range(1, PACK):
            gather_x(0, i, 0, S)
        load_wf(1, 0)
        load_wf(0, 1)
        load_wf(1, 1)
        gain_first_half(0)
        round_x0()
        gain_first_half(1)
        gain_chunk(2, 0, offset=PICKED_AT[0] + 8 * KIB)
        for i in range(PACK - 1):
            gather_x(1, i, 0, S)
        quantize_x0()
        gather_x(1, 3, 0, HALF)
        gather_x(1, 3, HALF, HALF)
        load_ws(0)
        load_ws(1)
        load_skip(0)
        load_skip(1)
        round_wf(0, 0, SCALAR)
        round_x1(0, SCALAR)
        round_x1(1, VECTOR)
        round_wf(1, 0, VECTOR)
        quantize_wf(0, 0)
        quantize_x1(0)
        quantize_wf(1, 0)
        round_wf(0, 1, VECTOR)
        quantize_x1(1)
        quantize_wf(0, 1)
        round_x1(2, SCALAR)
        round_x1(3, SCALAR)
        gain_chunk(3, 0)
        tanh_filter(0, 0)
        tanh_filter(1, 0)
        round_ws(0, 0, CHUNK, SCALAR)
        round_wf(1, 1, VECTOR)
        quantize_x1(2)
        quantize_wf(1, 1)
        gated_product(0, 0)
        tanh_filter(0, 1)
        tanh_filter(1, 1)
        gated_product(1, 0)
        quantize_h(0, 0)
        quantize_ws(0, 0)
        quantize_h(1, 0)
        quantize_x1(3)
        round_ws(1, 0, N, SCALAR)
        tanh_filter(2, 0)
        gated_product(0, 1)
        gated_product(1, 1)
        quantize_h(0, 1)
        quantize_h(1, 1)
        quantize_ws(1, 0)
        gated_product(2, 0)
        round_ws(0, CHUNK, CHUNK, SCALAR, X_AT[4])
        quantize_ws(0, CHUNK)
        quantize_h(2, 0)
        gain_chunk(3, 1, GPSIMD, X_AT[4])
        skip_sum(0, 0, stored=4)
        skip_sum(1, 0)
        skip_sum(0, 2, stored=4, passes=(1, 0))
        skip_sum(1, 2, passes=(1, 0))
        gain_chunk(2, 1)
        tanh_filter(2, 1)
        tanh_filter(3, 0)
        tanh_filter(3, 1)
        gated_product(2, 1)
        gated_product(3, 0)
        quantize_h(2, 1)
        quantize_h(3, 0)
        gated_product(3, 1)
        skip_sum(2, 0)
        quantize_h(3, 1)
        skip_sum(2, 2)
        skip_sum(3, 0, 1)
        skip_sum(3, 1, 1)
        skip_sum(3, 2, 1, "acc")
        skip_sum(3, 3, 1, "acc")
